import numpy as np
import ml_dtypes


def mxq(x, axis, fmt="e4m3"):
    dtype, down = {"e4m3": (ml_dtypes.float8_e4m3fn, 7), "e5m2": (ml_dtypes.float8_e5m2, 14)}[fmt]
    v = np.moveaxis(np.asarray(x, np.float32).astype(ml_dtypes.bfloat16).astype(np.float64), axis, -1)
    blocks = v.reshape(v.shape[:-1] + (-1, 32))
    amax = np.abs(blocks).max(-1, keepdims=True)
    byte = np.maximum(np.where(amax > 0, np.frexp(amax)[1] - 1 + 127, 0) - down, 1)
    scale = np.exp2(byte - 127.0)
    codes = (blocks / scale).astype(np.float32).astype(dtype).astype(np.float64)
    return np.moveaxis((codes * scale).reshape(v.shape), -1, axis)


WIDE = False


def mx_kscale(k):
    if not WIDE:
        return np.ones(k)
    levels = np.array([10, -10, 5, -5, 0])
    if k % 512:
        return np.exp2(np.random.permutation(np.resize(levels, k // 32))).repeat(32)
    a = np.empty((k // 512, 16))
    for p in range(k // 512):
        a[p, :8] = np.random.permutation(np.resize(levels, 8))
        for g in range(8):
            far = levels[np.abs(levels - a[p, g]) >= 10]
            a[p, g + 8] = far[np.random.randint(len(far))]
    return np.exp2(a.ravel()).repeat(32)


def f64(x):
    return np.asarray(x).astype(np.float64)


def striped(idx):
    return np.tile(idx.reshape(-1, 16).T, (8, 1)).astype(np.uint16)


def unstriped(offs):
    return offs[:16].T.reshape(-1).astype(np.int64)


E2M1 = np.array([0.0, 0.5, 1.0, 1.5, 2.0, 3.0, 4.0, 6.0, -0.0, -0.5, -1.0, -1.5, -2.0, -3.0, -4.0, -6.0])


def pack_weight(w, fmt):
    k, n = w.shape
    w = f64(np.asarray(w, np.float32).astype(ml_dtypes.bfloat16)).reshape(k // 32, 32, n)
    amax = np.abs(w).max(1)
    if fmt == "e4m3":
        byte = np.frexp(amax)[1] - 1 + 127 - 7
    else:
        mant, ex = np.frexp(amax / 6.0)
        byte = np.where(mant > 0.5, ex, ex - 1) + 127
    byte = np.clip(np.where(amax > 0, byte, 1), 1, 254)
    scaled = (w * np.exp2(127.0 - byte)[:, None, :]).reshape(k, n).astype(np.float32)
    by_word = np.ascontiguousarray(scaled.reshape(k // 512, 128, 4, n).transpose(0, 1, 3, 2))
    if fmt == "e4m3":
        words = by_word.astype(ml_dtypes.float8_e4m3fn).view(np.uint8)
    else:
        c = by_word.astype(ml_dtypes.float4_e2m1fn).view(np.uint8) & 0xF
        words = (c[..., 0::2] | (c[..., 1::2] << 4)).reshape(k // 512, 128, 2 * n)
    return np.ascontiguousarray(words), np.ascontiguousarray(byte.astype(np.uint8).reshape(k // 512, 16, n))


def unpack_weight(words, scales, fmt):
    g, _, n = scales.shape
    words = np.ascontiguousarray(words).reshape(g, 128, n, -1)
    if fmt == "e4m3":
        vals = words.view(ml_dtypes.float8_e4m3fn).astype(np.float64)
    else:
        nib = np.empty((g, 128, n, 4), np.uint8)
        nib[..., 0::2] = words & 0xF
        nib[..., 1::2] = words >> 4
        vals = E2M1[nib]
    vals = vals * np.repeat(np.exp2(scales.astype(np.float64) - 127.0), 8, axis=1)[..., None]
    return vals.transpose(0, 1, 3, 2).reshape(g * 512, n)


def gelu(v):
    return 0.5 * v * (1.0 + np.tanh(np.sqrt(2.0 / np.pi) * (v + 0.044715 * v**3)))


def striped8(idx):
    return np.concatenate([v.reshape(-1, 16).T for v in idx]).astype(np.uint16)


def unstriped8(offs):
    return np.stack([offs[16 * g:16 * g + 16].T.reshape(-1) for g in range(8)]).astype(np.int64)


def runs(v, idx8):
    k = np.arange(v.shape[0])
    return v[k[:, None], idx8[k % 512 // 64]]


K, K2, H, N, T, S, T2 = 1024, 512, 1024, 768, 2048, 512, 1024


def setup_inputs():
    n = np.random.standard_normal
    s = mx_kscale(K)[:, None]
    s2 = mx_kscale(K2)[:, None]
    u = mx_kscale(H)[:, None]
    tab_words, tab_scales = pack_weight(n((K, T)) * s, "e4m3")
    tab2_words, tab2_scales = pack_weight(n((K2, T)) * s2, "e4m3")
    w1_words, w1_scales = pack_weight(1.3 * n((K, H)) / np.sqrt(K) / s, "e2m1")
    w4_words, w4_scales = pack_weight(n((H, N)) / np.sqrt(H) / u, "e4m3")
    return {
        "tab_words": tab_words, "tab_scales": tab_scales,
        "tab2_words": tab2_words, "tab2_scales": tab2_scales,
        "offs": striped8(np.stack([np.random.permutation(T)[:S] for _ in range(8)])),
        "offs2": striped(np.random.permutation(T)[:S]),
        "offs3": striped(np.random.permutation(T2)[:S]),
        "w1_words": w1_words, "w1_scales": w1_scales,
        "w2": (0.38 * n((K, H)) / np.sqrt(K) / s).astype(np.float32),
        "phase": np.random.uniform(-1.0, 1.0, H).astype(np.float32),
        "gain": (np.random.uniform(1.0, 3.0, H) * u[:, 0]).astype(np.float32),
        "w3": (0.75 * n((K2, H)) / np.sqrt(K2) / s2 * u.T).astype(np.float32),
        "w4_words": w4_words, "w4_scales": w4_scales,
        "page1": n((N, T2)).astype(np.float32),
        "wgo": np.exp(0.3 * n((128, S))).astype(np.float32),
    }


def reference(tab_words, tab_scales, tab2_words, tab2_scales, offs, offs2, offs3, w1_words, w1_scales,
              w2, phase, gain, w3, w4_words, w4_scales, page1, wgo):
    v = runs(unpack_weight(tab_words, tab_scales, "e4m3"), unstriped8(offs))
    v2 = unpack_weight(tab2_words, tab2_scales, "e4m3")[:, unstriped(offs2)]
    a = unpack_weight(w1_words, w1_scales, "e2m1").T @ v
    b = mxq(f64(w2), 0, "e4m3").T @ v
    d = mxq(f64(w3), 0, "e4m3").T @ v2
    buzz = np.tanh(a) * np.sin(b + f64(phase)[:, None])
    h = buzz * f64(gain)[:, None] + d
    y = unpack_weight(w4_words, w4_scales, "e4m3").T @ mxq(h, 0, "e4m3")
    out = f64(page1).copy()
    out[:, unstriped(offs3)] = np.tile(f64(wgo), (N // 128, 1)) * y
    return out

@@ -1,0 +1,243 @@
+import math
+from contextlib import ExitStack
+
+import concourse.mybir as mybir
+
+K, K2, H, N, T, S, T2 = 1024, 512, 1024, 768, 2048, 512, 1024
+FLOPS = 2 * S * (2 * K * H + K2 * H + H * N)
+
+F32 = mybir.dt.float32
+BF16 = mybir.dt.bfloat16
+I32 = mybir.dt.int32
+U32 = mybir.dt.uint32
+U16 = mybir.dt.uint16
+U8 = mybir.dt.uint8
+FP8X4 = mybir.dt.float8_e4m3fn_x4
+FP4X4 = mybir.dt.float4_e2m1fn_x4
+ACT = mybir.ActivationFunctionType
+ALU = mybir.AluOpType
+
+P = 128
+PACK = 4
+KP = P * PACK
+TWO_PI = 2.0 * math.pi
+
+
+def tile_list_jawari_buzz_scores_kernel(tc, tab_words, tab_scales, tab2_words, tab2_scales, offs, offs2, offs3,
+                                                  w1_words, w1_scales, w2, phase, gain, w3, w4_words, w4_scales,
+                                                  page1, wgo, out):
+    nc = tc.nc
+    with ExitStack() as ctx:
+        keep = ctx.enter_context(tc.tile_pool(name="keep", bufs=1))
+        ring = ctx.enter_context(tc.tile_pool(name="ring", bufs=2))
+        psum = ctx.enter_context(tc.psum_pool(name="psum", bufs=2))
+
+        def held(name, shape, dtype, buffer=None):
+            return keep.tile(shape, dtype, name=name, tag=buffer or name, align_bytes=64)
+
+        lists = keep.tile([P, S // 16], U16, name="lists")
+        list2 = keep.tile([P, S // 16], U16, name="list2")
+        list3 = keep.tile([P, S // 16], U16, name="list3")
+
+        def load_scale_rows(queue, tile, first, rows):
+            for d in range(4):
+                queue.dma_start(tile[32 * d + first:32 * d + first + 4, :, :].bitcast(I32),
+                                rows[:, 4 * d:4 * d + 4, :].rearrange("a q n -> q a n").bitcast(I32))
+
+        raw, codes, scales, rounded, pages = {}, {}, {}, {}, {}
+
+        def load_chunk(name, w, a, b, buffer):
+            raw[name, a, b] = held("raw_%s_%d_%d" % (name, a, b), [P, PACK, KP], F32, buffer)
+            nc.sync.dma_start(raw[name, a, b][:],
+                              w[KP * a:KP * (a + 1), KP * b:KP * (b + 1)].rearrange("(p j) c -> p j c", j=PACK))
+
+        def load_table(name, words, buffer):
+            tile = held(name, [P, T], I32, buffer)
+            nc.sync.dma_start(tile[:], words.rearrange("p n t -> p (n t)").bitcast(I32))
+            return tile
+
+        def load_page(c, buffer):
+            pages[c] = held("page%d" % c, [P, T2], F32, buffer)
+            nc.sync.dma_start(pages[c][:], page1[P * c:P * (c + 1), :])
+
+        def round_chunk(key, copy):
+            rounded[key] = ring.tile([P, PACK, P, PACK], BF16, name="rounded", align_bytes=64, bufs=3)
+            copy(rounded[key][:].rearrange("p t m j -> p m j t"),
+                 raw[key][:].rearrange("p j (m t) -> p m j t", t=PACK))
+
+        def quantize_chunk(key):
+            codes[key] = held("codes_%s_%d_%d" % key, [P, KP], U32)
+            scales[key] = held("scales_%s_%d_%d" % key, [P, KP], U8)
+            nc.vector.quantize_mx(out=codes[key][:].bitcast(FP8X4), scales=scales[key][:],
+                                  in_=rounded[key][:].rearrange("p t m j -> p (t m j)"))
+
+        def gather_words(name, table, offsets):
+            tile = held(name, [P, S], U32)
+            nc.vector.tensor_copy(tile[:], table[:].bitcast(U32).indirect(offsets[:]))
+            return tile
+
+        tab_sc_both = held("tab_sc_both", [P, 2, T], U8, "buf_b")
+        w1_sc_raw = held("w1_sc_raw", [P, 2, H], U8)
+        tab2_sc = held("tab2_sc", [P, 1, T], U8)
+        v_sc = held("v_sc", [P, 2, S], U8)
+        w4_sc = held("w4_sc", [P, 2, N], U8)
+        nc.vector.memset(tab_sc_both[:].bitcast(I32), 0)
+        nc.gpsimd.memset(w1_sc_raw[:].bitcast(I32), 0)
+        nc.vector.memset(tab2_sc[:].bitcast(I32), 0)
+        nc.vector.memset(v_sc[:].bitcast(I32), 0)
+        nc.vector.memset(w4_sc[:].bitcast(I32), 0)
+
+        nc.sync.dma_start(lists[:], offs)
+        nc.sync.dma_start(list2[:], offs2)
+        nc.sync.dma_start(list3[:], offs3)
+        w1_raw = held("w1_raw", [P, 2, 2 * H], U8, "buf_a")
+        nc.sync.dma_start(w1_raw[:].bitcast(I32), w1_words.rearrange("a p n -> p a n").bitcast(I32))
+        tab0 = load_table("tab0", tab_words[0], "buf_c")
+        load_scale_rows(nc.scalar, tab_sc_both, 14, tab_scales)
+        load_scale_rows(nc.scalar, w1_sc_raw, 0, w1_scales)
+        phase_sb = held("phase_sb", [P, 2, PACK], F32)
+        gain_sb = held("gain_sb", [P, 2, PACK], F32)
+        nc.gpsimd.dma_start(phase_sb[:], phase.rearrange("(b p t) -> p b t", b=2, t=PACK))
+        load_scale_rows(nc.gpsimd, tab2_sc, 0, tab2_scales)
+        nc.gpsimd.dma_start(gain_sb[:], gain.rearrange("(b p t) -> p b t", b=2, t=PACK))
+        load_scale_rows(nc.gpsimd, w4_sc, 0, w4_scales)
+
+        w1_w = held("w1_w", [P, 2, 2 * H], U8, "buf_f")
+        w1_sc = held("w1_sc", [P, 2, H], U8)
+        nc.vector.tensor_copy(
+            w1_w[:].bitcast(U16).rearrange("p a (b t m) -> p (a b) m t", b=2, t=PACK),
+            w1_raw[:].bitcast(U16).rearrange("p a (b m t) -> p (a b) m t", b=2, t=PACK))
+        tab1 = load_table("tab1", tab_words[1], "buf_a")
+
+        tab_sc = [held("tab_sc0", [P, T], U8, "buf_d"), held("tab_sc1", [P, T], U8)]
+        picked_sc = held("picked_sc", [P, 2, S], U8)
+        for a in range(2):
+            nc.vector.tensor_copy(tab_sc[a][:].bitcast(I32), tab_sc_both[:, a, :].bitcast(I32))
+        load_chunk("w2", w2, 0, 0, "buf_b")
+        for a in range(2):
+            nc.vector.tensor_copy(picked_sc[:, a, :], tab_sc[a][:].indirect(lists[:]))
+        load_chunk("w2", w2, 1, 0, "buf_d")
+        nc.scalar.dma_start(v_sc[0:100, :, :].bitcast(I32), picked_sc[14:114, :, :].bitcast(I32))
+
+        v_w = [gather_words("v_w0", tab0, lists)]
+        load_chunk("w2", w2, 0, 1, "buf_c")
+        v_w.append(gather_words("v_w1", tab1, lists))
+        load_chunk("w2", w2, 1, 1, "buf_a")
+        nc.vector.tensor_copy(
+            w1_sc[:].rearrange("p a (b t m) -> p (a b) m t", b=2, t=PACK),
+            w1_sc_raw[:].rearrange("p a (b m t) -> p (a b) m t", b=2, t=PACK))
+        round_chunk(("w2", 0, 0), nc.scalar.copy)
+        tab2 = load_table("tab2", tab2_words[0], "buf_b")
+        turned = held("turned", [P, 2, PACK], F32)
+        nc.vector.tensor_scalar(turned[:], phase_sb[:], TWO_PI, None, ALU.add)
+
+        tanh_a = held("tanh_a", [P, 2 * PACK, S], F32)
+
+        def tanh_slice(s):
+            acc = psum.tile([P, S], F32, name="acc_a")
+            for a in range(2):
+                nc.tensor.matmul_mx(out=acc[:], lhsT=w1_w[:, a, 2 * P * s:2 * P * (s + 1)].bitcast(FP4X4),
+                                    lhsT_scale=w1_sc[:, a, P * s:P * (s + 1)],
+                                    rhs=v_w[a][:].bitcast(FP8X4), rhs_scale=v_sc[:, a, :],
+                                    start=(a == 0), stop=(a == 1))
+            nc.scalar.activation(tanh_a[:, s, :], acc[:], ACT.Tanh)
+
+        sines = {}
+
+        def sine_slice(b, t):
+            acc = psum.tile([P, S], F32, name="acc_b")
+            for a in range(2):
+                key = ("w2", a, b)
+                nc.tensor.matmul_mx(out=acc[:], lhsT=codes[key][:, P * t:P * (t + 1)].bitcast(FP8X4),
+                                    lhsT_scale=scales[key][:, P * t:P * (t + 1)],
+                                    rhs=v_w[a][:].bitcast(FP8X4), rhs_scale=v_sc[:, a, :],
+                                    start=(a == 0), stop=(a == 1))
+            turns = ring.tile([P, S], I32, name="turns")
+            nc.vector.tensor_scalar(turns[:], acc[:], turned[:, b, t:t + 1], 1.0 / TWO_PI, ALU.add, ALU.mult)
+            rest = ring.tile([P, S], F32, name="rest", bufs=4)
+            nc.vector.scalar_tensor_tensor(rest[:], turns[:], -TWO_PI, acc[:], ALU.mult, ALU.add)
+            sines[b, t] = ring.tile([P, S], F32, name="sine", bufs=4)
+            nc.scalar.activation(sines[b, t][:], rest[:], ACT.Sin, bias=turned[:, b, t:t + 1])
+
+        def product_slice(b, t):
+            s = PACK * b + t
+            nc.vector.tensor_tensor(tanh_a[:, s, :], tanh_a[:, s, :], sines[b, t][:], ALU.mult)
+
+        h_rows = [held("h_rows%d" % b, [P, PACK, S], BF16) for b in range(2)]
+        h_woven = [held("h_woven%d" % b, [P, S, PACK], BF16) for b in range(2)]
+        h_w = [held("h_w%d" % b, [P, S], U32) for b in range(2)]
+        h_sc = [held("h_sc%d" % b, [P, S], U8) for b in range(2)]
+
+        def sum_slice(b, t):
+            key = ("w3", 0, b)
+            acc = psum.tile([P, S], F32, name="acc_d")
+            nc.tensor.matmul_mx(out=acc[:], lhsT=codes[key][:, P * t:P * (t + 1)].bitcast(FP8X4),
+                                lhsT_scale=scales[key][:, P * t:P * (t + 1)],
+                                rhs=v2_w[:].bitcast(FP8X4), rhs_scale=v2_sc[:], start=True, stop=True)
+            nc.vector.scalar_tensor_tensor(h_rows[b][:, t, :], tanh_a[:, PACK * b + t, :], gain_sb[:, b, t:t + 1],
+                                           acc[:], ALU.mult, ALU.add)
+
+        def weave_h(b, copy):
+            copy(h_woven[b][:].rearrange("p (c i) t -> p c t i", i=4),
+                 h_rows[b][:].rearrange("p t (c i) -> p c t i", i=4))
+
+        def quantize_h(b):
+            nc.vector.quantize_mx(out=h_w[b][:].bitcast(FP8X4), scales=h_sc[b][:],
+                                  in_=h_woven[b][:].rearrange("p n t -> p (n t)"))
+
+        round_chunk(("w2", 1, 0), nc.vector.tensor_copy)
+        load_chunk("w3", w3, 0, 0, "buf_d")
+        quantize_chunk(("w2", 0, 0))
+        quantize_chunk(("w2", 1, 0))
+        v2_sc = held("v2_sc", [P, S], U8)
+        nc.vector.tensor_copy(v2_sc[:], tab2_sc[:, 0, :].indirect(list2[:]))
+        for s in range(2 * PACK):
+            tanh_slice(s)
+        load_chunk("w3", w3, 0, 1, "buf_f")
+        round_chunk(("w2", 0, 1), nc.scalar.copy)
+        w4_w = held("w4_w", [P, 2, N], I32, "buf_c")
+        nc.sync.dma_start(w4_w[:], w4_words.rearrange("a p n t -> p a (n t)").bitcast(I32))
+        for t in range(PACK):
+            sine_slice(0, t)
+        round_chunk(("w2", 1, 1), nc.scalar.copy)
+        load_page(0, "buf_a")
+        quantize_chunk(("w2", 0, 1))
+        for t in range(PACK):
+            product_slice(0, t)
+        quantize_chunk(("w2", 1, 1))
+        v2_w = gather_words("v2_w", tab2, list2)
+        load_page(1, "buf_b")
+        round_chunk(("w3", 0, 0), nc.scalar.copy)
+        load_page(2, "buf_d")
+        for t in range(PACK):
+            sine_slice(1, t)
+        wgo_sb = held("wgo_sb", [P, S], F32, "v_w0")
+        nc.sync.dma_start(wgo_sb[:], wgo)
+        load_page(3, "v_w1")
+        quantize_chunk(("w3", 0, 0))
+        round_chunk(("w3", 0, 1), nc.scalar.copy)
+        load_page(4, "buf_f")
+        for t in range(PACK):
+            sum_slice(0, t)
+        weave_h(0, nc.scalar.copy)
+        load_page(5, "h_rows0")
+        for t in range(PACK):
+            product_slice(1, t)
+        quantize_chunk(("w3", 0, 1))
+        for t in range(PACK):
+            sum_slice(1, t)
+        quantize_h(0)
+        weave_h(1, nc.vector.tensor_copy)
+        quantize_h(1)
+
+        for c in range(N // P):
+            acc = psum.tile([P, S], F32, name="acc_y")
+            for b in range(2):
+                nc.tensor.matmul_mx(out=acc[:], lhsT=w4_w[:, b, P * c:P * (c + 1)].bitcast(FP8X4),
+                                    lhsT_scale=w4_sc[:, b, P * c:P * (c + 1)],
+                                    rhs=h_w[b][:].bitcast(FP8X4), rhs_scale=h_sc[b][:],
+                                    start=(b == 0), stop=(b == 1))
+            scores = ring.tile([P, S], F32, name="scores", bufs=3)
+            nc.scalar.copy(scores[:], acc[:])
+            nc.vector.tensor_tensor(pages[c][:].indirect(list3[:]), scores[:], wgo_sb[:], ALU.mult)
+            nc.sync.dma_start(out[P * c:P * (c + 1), :], pages[c][:])

@@ -39,25 +39,25 @@ def tile_list_jawari_buzz_scores_kernel(tc, tab_words, tab_scales, tab2_words, t
         list2 = keep.tile([P, S // 16], U16, name="list2")
         list3 = keep.tile([P, S // 16], U16, name="list3")
 
-        def load_scale_rows(queue, tile, first, rows):
-            for d in range(4):
+        def load_scale_rows(queue, tile, first, rows, quadrants=range(4)):
+            for d in quadrants:
                 queue.dma_start(tile[32 * d + first:32 * d + first + 4, :, :].bitcast(I32),
                                 rows[:, 4 * d:4 * d + 4, :].rearrange("a q n -> q a n").bitcast(I32))
 
         raw, codes, scales, rounded, pages = {}, {}, {}, {}, {}
 
-        def load_chunk(name, w, a, b, buffer):
-            raw[name, a, b] = held("raw_%s_%d_%d" % (name, a, b), [P, PACK, KP], F32, buffer)
+        def load_chunk(name, w, a, b):
+            raw[name, a, b] = held("raw_%s_%d_%d" % (name, a, b), [P, PACK, KP], F32)
             nc.sync.dma_start(raw[name, a, b][:],
                               w[KP * a:KP * (a + 1), KP * b:KP * (b + 1)].rearrange("(p j) c -> p j c", j=PACK))
 
-        def load_table(name, words, buffer):
-            tile = held(name, [P, T], I32, buffer)
+        def load_table(name, words):
+            tile = held(name, [P, T], I32)
             nc.sync.dma_start(tile[:], words.rearrange("p n t -> p (n t)").bitcast(I32))
             return tile
 
-        def load_page(c, buffer):
-            pages[c] = held("page%d" % c, [P, T2], F32, buffer)
+        def load_page(c):
+            pages[c] = held("page%d" % c, [P, T2], F32)
             nc.sync.dma_start(pages[c][:], page1[P * c:P * (c + 1), :])
 
         def round_chunk(key, copy):
@@ -71,70 +71,83 @@ def tile_list_jawari_buzz_scores_kernel(tc, tab_words, tab_scales, tab2_words, t
             nc.vector.quantize_mx(out=codes[key][:].bitcast(FP8X4), scales=scales[key][:],
                                   in_=rounded[key][:].rearrange("p t m j -> p (t m j)"))
 
-        def gather_words(name, table, offsets):
-            tile = held(name, [P, S], U32)
+        def gather_words(name, table, offsets, buffer=None):
+            tile = held(name, [P, S], U32, buffer)
             nc.vector.tensor_copy(tile[:], table[:].bitcast(U32).indirect(offsets[:]))
             return tile
 
-        tab_sc_both = held("tab_sc_both", [P, 2, T], U8, "buf_b")
+        tab_sc_both = held("tab_sc_both", [P, 2, T], U8)
         w1_sc_raw = held("w1_sc_raw", [P, 2, H], U8)
         tab2_sc = held("tab2_sc", [P, 1, T], U8)
-        v_sc = held("v_sc", [P, 2, S], U8)
         w4_sc = held("w4_sc", [P, 2, N], U8)
-        nc.vector.memset(tab_sc_both[:].bitcast(I32), 0)
-        nc.gpsimd.memset(w1_sc_raw[:].bitcast(I32), 0)
-        nc.vector.memset(tab2_sc[:].bitcast(I32), 0)
+        v_sc = held("v_sc", [P, 2, S], U8)
+        zero = held("zero", [P, 1], F32)
+        nc.gpsimd.memset(tab_sc_both[:, 1, :].bitcast(I32), 0)
+        nc.vector.memset(tab_sc_both[:, 0, :].bitcast(I32), 0)
+        nc.vector.memset(w1_sc_raw[:].bitcast(I32), 0)
+        nc.vector.memset(zero[:], 0.0)
         nc.vector.memset(v_sc[:].bitcast(I32), 0)
+        nc.vector.memset(tab2_sc[:].bitcast(I32), 0)
         nc.vector.memset(w4_sc[:].bitcast(I32), 0)
 
-        nc.sync.dma_start(lists[:], offs)
-        nc.sync.dma_start(list2[:], offs2)
-        nc.sync.dma_start(list3[:], offs3)
-        w1_raw = held("w1_raw", [P, 2, 2 * H], U8, "buf_a")
-        nc.sync.dma_start(w1_raw[:].bitcast(I32), w1_words.rearrange("a p n -> p a n").bitcast(I32))
-        tab0 = load_table("tab0", tab_words[0], "buf_c")
         load_scale_rows(nc.scalar, tab_sc_both, 14, tab_scales)
         load_scale_rows(nc.scalar, w1_sc_raw, 0, w1_scales)
+        unread = held("unread", [P, 1], F32)
+        nc.scalar.activation(unread[:], zero[:], ACT.Silu)
+
+        w1_raw = held("w1_raw", [P, 2, 2 * H], U8)
+        nc.sync.dma_start(w1_raw[:].bitcast(I32), w1_words.rearrange("a p n -> p a n").bitcast(I32))
+        nc.sync.dma_start(lists[:], offs)
         phase_sb = held("phase_sb", [P, 2, PACK], F32)
         gain_sb = held("gain_sb", [P, 2, PACK], F32)
-        nc.gpsimd.dma_start(phase_sb[:], phase.rearrange("(b p t) -> p b t", b=2, t=PACK))
-        load_scale_rows(nc.gpsimd, tab2_sc, 0, tab2_scales)
-        nc.gpsimd.dma_start(gain_sb[:], gain.rearrange("(b p t) -> p b t", b=2, t=PACK))
-        load_scale_rows(nc.gpsimd, w4_sc, 0, w4_scales)
+        tab0 = load_table("tab0", tab_words[0])
+        tab1 = load_table("tab1", tab_words[1])
+        load_chunk("w2", w2, 0, 0)
+        load_chunk("w2", w2, 1, 0)
+        nc.sync.dma_start(phase_sb[:], phase.rearrange("(b p t) -> p b t", b=2, t=PACK))
+        load_chunk("w2", w2, 0, 1)
+        nc.sync.dma_start(list2[:], offs2)
+        load_scale_rows(nc.sync, tab2_sc, 0, tab2_scales, range(2))
+        load_chunk("w2", w2, 1, 1)
+        load_scale_rows(nc.sync, tab2_sc, 0, tab2_scales, range(2, 4))
+        tab2 = load_table("tab2", tab2_words[0])
+        nc.sync.dma_start(gain_sb[:], gain.rearrange("(b p t) -> p b t", b=2, t=PACK))
+        load_chunk("w3", w3, 0, 0)
+        load_chunk("w3", w3, 0, 1)
+        w4_w = held("w4_w", [P, 2, N], I32)
+        nc.sync.dma_start(w4_w[:], w4_words.rearrange("a p n t -> p a (n t)").bitcast(I32))
+        load_scale_rows(nc.sync, w4_sc, 0, w4_scales)
+        nc.sync.dma_start(list3[:], offs3)
+        wgo_sb = held("wgo_sb", [P, S], F32)
+        nc.sync.dma_start(wgo_sb[:], wgo)
+        for c in range(N // P):
+            load_page(c)
 
-        w1_w = held("w1_w", [P, 2, 2 * H], U8, "buf_f")
-        w1_sc = held("w1_sc", [P, 2, H], U8)
+        w1_w = held("w1_w", [P, 2, 2 * H], U8)
         nc.vector.tensor_copy(
             w1_w[:].bitcast(U16).rearrange("p a (b t m) -> p (a b) m t", b=2, t=PACK),
             w1_raw[:].bitcast(U16).rearrange("p a (b m t) -> p (a b) m t", b=2, t=PACK))
-        tab1 = load_table("tab1", tab_words[1], "buf_a")
 
-        tab_sc = [held("tab_sc0", [P, T], U8, "buf_d"), held("tab_sc1", [P, T], U8)]
+        tab_sc = [held("tab_sc%d" % a, [P, T], U8) for a in range(2)]
         picked_sc = held("picked_sc", [P, 2, S], U8)
         for a in range(2):
             nc.vector.tensor_copy(tab_sc[a][:].bitcast(I32), tab_sc_both[:, a, :].bitcast(I32))
-        load_chunk("w2", w2, 0, 0, "buf_b")
         for a in range(2):
             nc.vector.tensor_copy(picked_sc[:, a, :], tab_sc[a][:].indirect(lists[:]))
-        load_chunk("w2", w2, 1, 0, "buf_d")
         nc.scalar.dma_start(v_sc[0:100, :, :].bitcast(I32), picked_sc[14:114, :, :].bitcast(I32))
 
-        v_w = [gather_words("v_w0", tab0, lists)]
-        load_chunk("w2", w2, 0, 1, "buf_c")
-        v_w.append(gather_words("v_w1", tab1, lists))
-        load_chunk("w2", w2, 1, 1, "buf_a")
+        v_w = [gather_words("v_w0", tab0, lists, "tab_sc0")]
+        w1_sc = held("w1_sc", [P, 2, H], U8, "tab_sc1")
         nc.vector.tensor_copy(
             w1_sc[:].rearrange("p a (b t m) -> p (a b) m t", b=2, t=PACK),
             w1_sc_raw[:].rearrange("p a (b m t) -> p (a b) m t", b=2, t=PACK))
+        v_w.append(gather_words("v_w1", tab1, lists))
         round_chunk(("w2", 0, 0), nc.scalar.copy)
-        tab2 = load_table("tab2", tab2_words[0], "buf_b")
-        turned = held("turned", [P, 2, PACK], F32)
-        nc.vector.tensor_scalar(turned[:], phase_sb[:], TWO_PI, None, ALU.add)
 
         tanh_a = held("tanh_a", [P, 2 * PACK, S], F32)
 
         def tanh_slice(s):
-            acc = psum.tile([P, S], F32, name="acc_a")
+            acc = psum.tile([P, S], F32, name="acc_a", bufs=2)
             for a in range(2):
                 nc.tensor.matmul_mx(out=acc[:], lhsT=w1_w[:, a, 2 * P * s:2 * P * (s + 1)].bitcast(FP4X4),
                                     lhsT_scale=w1_sc[:, a, P * s:P * (s + 1)],
@@ -145,99 +158,95 @@ def tile_list_jawari_buzz_scores_kernel(tc, tab_words, tab_scales, tab2_words, t
         sines = {}
 
         def sine_slice(b, t):
-            acc = psum.tile([P, S], F32, name="acc_b")
+            acc = psum.tile([P, S], F32, name="acc_b", bufs=3)
             for a in range(2):
                 key = ("w2", a, b)
                 nc.tensor.matmul_mx(out=acc[:], lhsT=codes[key][:, P * t:P * (t + 1)].bitcast(FP8X4),
                                     lhsT_scale=scales[key][:, P * t:P * (t + 1)],
                                     rhs=v_w[a][:].bitcast(FP8X4), rhs_scale=v_sc[:, a, :],
                                     start=(a == 0), stop=(a == 1))
-            turns = ring.tile([P, S], I32, name="turns")
-            nc.vector.tensor_scalar(turns[:], acc[:], turned[:, b, t:t + 1], 1.0 / TWO_PI, ALU.add, ALU.mult)
-            rest = ring.tile([P, S], F32, name="rest", bufs=4)
+            turns = ring.tile([P, S], I32, name="turns", bufs=3)
+            nc.vector.tensor_scalar(turns[:], acc[:], phase_sb[:, b, t:t + 1], 1.0 / TWO_PI, ALU.add, ALU.mult)
+            rest = ring.tile([P, S], F32, name="rest", bufs=8)
             nc.vector.scalar_tensor_tensor(rest[:], turns[:], -TWO_PI, acc[:], ALU.mult, ALU.add)
-            sines[b, t] = ring.tile([P, S], F32, name="sine", bufs=4)
-            nc.scalar.activation(sines[b, t][:], rest[:], ACT.Sin, bias=turned[:, b, t:t + 1])
+            sines[b, t] = rest
+            nc.scalar.activation(sines[b, t][:], rest[:], ACT.Sin, bias=phase_sb[:, b, t:t + 1])
 
         def product_slice(b, t):
             s = PACK * b + t
-            nc.vector.tensor_tensor(tanh_a[:, s, :], tanh_a[:, s, :], sines[b, t][:], ALU.mult)
+            nc.gpsimd.tensor_tensor(tanh_a[:, s, :], tanh_a[:, s, :], sines[b, t][:], ALU.mult)
 
-        h_rows = [held("h_rows%d" % b, [P, PACK, S], BF16) for b in range(2)]
-        h_woven = [held("h_woven%d" % b, [P, S, PACK], BF16) for b in range(2)]
-        h_w = [held("h_w%d" % b, [P, S], U32) for b in range(2)]
-        h_sc = [held("h_sc%d" % b, [P, S], U8) for b in range(2)]
+        W = S // 1
+        h_rows, h_woven, h_w, h_sc = {}, {}, {}, {}
 
-        def sum_slice(b, t):
+        def sum_slice(b, t, g):
             key = ("w3", 0, b)
-            acc = psum.tile([P, S], F32, name="acc_d")
+            cols = slice(W * g, W * (g + 1))
+            if t == 0:
+                h_rows[b, g] = held("h_rows%d%d" % (b, g), [P, PACK, W], BF16)
+            acc = psum.tile([P, W], F32, name="acc_d", bufs=3)
             nc.tensor.matmul_mx(out=acc[:], lhsT=codes[key][:, P * t:P * (t + 1)].bitcast(FP8X4),
                                 lhsT_scale=scales[key][:, P * t:P * (t + 1)],
-                                rhs=v2_w[:].bitcast(FP8X4), rhs_scale=v2_sc[:], start=True, stop=True)
-            nc.vector.scalar_tensor_tensor(h_rows[b][:, t, :], tanh_a[:, PACK * b + t, :], gain_sb[:, b, t:t + 1],
+                                rhs=v2_w[:, cols].bitcast(FP8X4), rhs_scale=v2_sc[:, cols], start=True, stop=True)
+            nc.vector.scalar_tensor_tensor(h_rows[b, g][:, t, :], tanh_a[:, PACK * b + t, cols], gain_sb[:, b, t:t + 1],
                                            acc[:], ALU.mult, ALU.add)
 
-        def weave_h(b, copy):
-            copy(h_woven[b][:].rearrange("p (c i) t -> p c t i", i=4),
-                 h_rows[b][:].rearrange("p t (c i) -> p c t i", i=4))
+        def weave_h(b, g, copy):
+            h_woven[b, g] = held("h_woven%d%d" % (b, g), [P, W, PACK], BF16)
+            copy(h_woven[b, g][:].rearrange("p (c i) t -> p c t i", i=4),
+                 h_rows[b, g][:].rearrange("p t (c i) -> p c t i", i=4))
 
-        def quantize_h(b):
-            nc.vector.quantize_mx(out=h_w[b][:].bitcast(FP8X4), scales=h_sc[b][:],
-                                  in_=h_woven[b][:].rearrange("p n t -> p (n t)"))
+        def quantize_h(b, g):
+            h_w[b, g] = held("h_w%d%d" % (b, g), [P, W], U32)
+            h_sc[b, g] = held("h_sc%d%d" % (b, g), [P, W], U8)
+            nc.vector.quantize_mx(out=h_w[b, g][:].bitcast(FP8X4), scales=h_sc[b, g][:],
+                                  in_=h_woven[b, g][:].rearrange("p n t -> p (n t)"))
+
+        def score_page(c, g):
+            cols = slice(W * g, W * (g + 1))
+            acc = psum.tile([P, W], F32, name="acc_y", tag="acc_d", bufs=3)
+            for b in range(2):
+                nc.tensor.matmul_mx(out=acc[:], lhsT=w4_w[:, b, P * c:P * (c + 1)].bitcast(FP8X4),
+                                    lhsT_scale=w4_sc[:, b, P * c:P * (c + 1)],
+                                    rhs=h_w[b, g][:].bitcast(FP8X4), rhs_scale=h_sc[b, g][:],
+                                    start=(b == 0), stop=(b == 1))
+            scores = ring.tile([P, W], F32, name="scores", bufs=3)
+            nc.scalar.copy(scores[:], acc[:])
+            nc.vector.tensor_tensor(pages[c][:].indirect(list3[:, W // 16 * g:W // 16 * (g + 1)]), scores[:],
+                                    wgo_sb[:, cols], ALU.mult)
 
         round_chunk(("w2", 1, 0), nc.vector.tensor_copy)
-        load_chunk("w3", w3, 0, 0, "buf_d")
         quantize_chunk(("w2", 0, 0))
         quantize_chunk(("w2", 1, 0))
-        v2_sc = held("v2_sc", [P, S], U8)
-        nc.vector.tensor_copy(v2_sc[:], tab2_sc[:, 0, :].indirect(list2[:]))
-        for s in range(2 * PACK):
-            tanh_slice(s)
-        load_chunk("w3", w3, 0, 1, "buf_f")
-        round_chunk(("w2", 0, 1), nc.scalar.copy)
-        w4_w = held("w4_w", [P, 2, N], I32, "buf_c")
-        nc.sync.dma_start(w4_w[:], w4_words.rearrange("a p n t -> p a (n t)").bitcast(I32))
         for t in range(PACK):
             sine_slice(0, t)
+            tanh_slice(t)
+        round_chunk(("w2", 0, 1), nc.scalar.copy)
         round_chunk(("w2", 1, 1), nc.scalar.copy)
-        load_page(0, "buf_a")
         quantize_chunk(("w2", 0, 1))
         for t in range(PACK):
             product_slice(0, t)
         quantize_chunk(("w2", 1, 1))
-        v2_w = gather_words("v2_w", tab2, list2)
-        load_page(1, "buf_b")
-        round_chunk(("w3", 0, 0), nc.scalar.copy)
-        load_page(2, "buf_d")
         for t in range(PACK):
             sine_slice(1, t)
-        wgo_sb = held("wgo_sb", [P, S], F32, "v_w0")
-        nc.sync.dma_start(wgo_sb[:], wgo)
-        load_page(3, "v_w1")
+            tanh_slice(PACK + t)
+        v2_sc = held("v2_sc", [P, S], U8)
+        nc.vector.tensor_copy(v2_sc[:], tab2_sc[:, 0, :].indirect(list2[:]))
+        v2_w = gather_words("v2_w", tab2, list2)
+        round_chunk(("w3", 0, 0), nc.scalar.copy)
         quantize_chunk(("w3", 0, 0))
         round_chunk(("w3", 0, 1), nc.scalar.copy)
-        load_page(4, "buf_f")
-        for t in range(PACK):
-            sum_slice(0, t)
-        weave_h(0, nc.scalar.copy)
-        load_page(5, "h_rows0")
         for t in range(PACK):
             product_slice(1, t)
         quantize_chunk(("w3", 0, 1))
-        for t in range(PACK):
-            sum_slice(1, t)
-        quantize_h(0)
-        weave_h(1, nc.vector.tensor_copy)
-        quantize_h(1)
-
-        for c in range(N // P):
-            acc = psum.tile([P, S], F32, name="acc_y")
+        for g in range(1):
             for b in range(2):
-                nc.tensor.matmul_mx(out=acc[:], lhsT=w4_w[:, b, P * c:P * (c + 1)].bitcast(FP8X4),
-                                    lhsT_scale=w4_sc[:, b, P * c:P * (c + 1)],
-                                    rhs=h_w[b][:].bitcast(FP8X4), rhs_scale=h_sc[b][:],
-                                    start=(b == 0), stop=(b == 1))
-            scores = ring.tile([P, S], F32, name="scores", bufs=3)
-            nc.scalar.copy(scores[:], acc[:])
-            nc.vector.tensor_tensor(pages[c][:].indirect(list3[:]), scores[:], wgo_sb[:], ALU.mult)
+                for t in range(PACK):
+                    sum_slice(b, t, g)
+                weave_h(b, g, nc.vector.tensor_copy if b else nc.scalar.copy)
+            for b in range(2):
+                quantize_h(b, g)
+        for c in range(N // P):
+            for g in range(1):
+                score_page(c, g)
             nc.sync.dma_start(out[P * c:P * (c + 1), :], pages[c][:])

@@ -29,6 +29,7 @@ def tile_list_jawari_buzz_scores_kernel(tc, tab_words, tab_scales, tab2_words, t
     nc = tc.nc
     with ExitStack() as ctx:
         keep = ctx.enter_context(tc.tile_pool(name="keep", bufs=1))
+        early = ctx.enter_context(tc.tile_pool(name="early", bufs=1))
         ring = ctx.enter_context(tc.tile_pool(name="ring", bufs=2))
         psum = ctx.enter_context(tc.psum_pool(name="psum", bufs=2))
 
@@ -71,8 +72,7 @@ def tile_list_jawari_buzz_scores_kernel(tc, tab_words, tab_scales, tab2_words, t
             nc.vector.quantize_mx(out=codes[key][:].bitcast(FP8X4), scales=scales[key][:],
                                   in_=rounded[key][:].rearrange("p t m j -> p (t m j)"))
 
-        def gather_words(name, table, offsets, buffer=None):
-            tile = held(name, [P, S], U32, buffer)
+        def gather_words(tile, table, offsets):
             nc.vector.tensor_copy(tile[:], table[:].bitcast(U32).indirect(offsets[:]))
             return tile
 
@@ -91,25 +91,26 @@ def tile_list_jawari_buzz_scores_kernel(tc, tab_words, tab_scales, tab2_words, t
         nc.vector.memset(w4_sc[:].bitcast(I32), 0)
 
         load_scale_rows(nc.scalar, tab_sc_both, 14, tab_scales)
-        load_scale_rows(nc.scalar, w1_sc_raw, 0, w1_scales)
         unread = held("unread", [P, 1], F32)
         nc.scalar.activation(unread[:], zero[:], ACT.Silu)
 
-        w1_raw = held("w1_raw", [P, 2, 2 * H], U8)
+        w1_raw = early.tile([P, 2, 2 * H], U8, name="w1_raw", align_bytes=64, offset=0)
         nc.sync.dma_start(w1_raw[:].bitcast(I32), w1_words.rearrange("a p n -> p a n").bitcast(I32))
         nc.sync.dma_start(lists[:], offs)
         phase_sb = held("phase_sb", [P, 2, PACK], F32)
         gain_sb = held("gain_sb", [P, 2, PACK], F32)
-        tab0 = load_table("tab0", tab_words[0])
-        tab1 = load_table("tab1", tab_words[1])
         load_chunk("w2", w2, 0, 0)
+        tab0 = load_table("tab0", tab_words[0])
+        load_scale_rows(nc.sync, w1_sc_raw, 0, w1_scales, range(2))
+        tab1 = load_table("tab1", tab_words[1])
+        load_scale_rows(nc.sync, w1_sc_raw, 0, w1_scales, range(2, 4))
         load_chunk("w2", w2, 1, 0)
         nc.sync.dma_start(phase_sb[:], phase.rearrange("(b p t) -> p b t", b=2, t=PACK))
-        load_chunk("w2", w2, 0, 1)
         nc.sync.dma_start(list2[:], offs2)
+        load_chunk("w2", w2, 0, 1)
         load_scale_rows(nc.sync, tab2_sc, 0, tab2_scales, range(2))
-        load_chunk("w2", w2, 1, 1)
         load_scale_rows(nc.sync, tab2_sc, 0, tab2_scales, range(2, 4))
+        load_chunk("w2", w2, 1, 1)
         tab2 = load_table("tab2", tab2_words[0])
         nc.sync.dma_start(gain_sb[:], gain.rearrange("(b p t) -> p b t", b=2, t=PACK))
         load_chunk("w3", w3, 0, 0)
@@ -128,7 +129,7 @@ def tile_list_jawari_buzz_scores_kernel(tc, tab_words, tab_scales, tab2_words, t
             w1_w[:].bitcast(U16).rearrange("p a (b t m) -> p (a b) m t", b=2, t=PACK),
             w1_raw[:].bitcast(U16).rearrange("p a (b m t) -> p (a b) m t", b=2, t=PACK))
 
-        tab_sc = [held("tab_sc%d" % a, [P, T], U8) for a in range(2)]
+        tab_sc = [early.tile([P, T], U8, name="tab_sc%d" % a, align_bytes=64, offset=T * a) for a in range(2)]
         picked_sc = held("picked_sc", [P, 2, S], U8)
         for a in range(2):
             nc.vector.tensor_copy(tab_sc[a][:].bitcast(I32), tab_sc_both[:, a, :].bitcast(I32))
@@ -136,18 +137,18 @@ def tile_list_jawari_buzz_scores_kernel(tc, tab_words, tab_scales, tab2_words, t
             nc.vector.tensor_copy(picked_sc[:, a, :], tab_sc[a][:].indirect(lists[:]))
         nc.scalar.dma_start(v_sc[0:100, :, :].bitcast(I32), picked_sc[14:114, :, :].bitcast(I32))
 
-        v_w = [gather_words("v_w0", tab0, lists, "tab_sc0")]
-        w1_sc = held("w1_sc", [P, 2, H], U8, "tab_sc1")
+        v_w = [gather_words(early.tile([P, S], U32, name="v_w0", align_bytes=64, offset=0), tab0, lists)]
+        w1_sc = early.tile([P, 2, H], U8, name="w1_sc", align_bytes=64, offset=T)
         nc.vector.tensor_copy(
             w1_sc[:].rearrange("p a (b t m) -> p (a b) m t", b=2, t=PACK),
             w1_sc_raw[:].rearrange("p a (b m t) -> p (a b) m t", b=2, t=PACK))
-        v_w.append(gather_words("v_w1", tab1, lists))
+        v_w.append(gather_words(held("v_w1", [P, S], U32), tab1, lists))
         round_chunk(("w2", 0, 0), nc.scalar.copy)
 
         tanh_a = held("tanh_a", [P, 2 * PACK, S], F32)
 
         def tanh_slice(s):
-            acc = psum.tile([P, S], F32, name="acc_a", bufs=2)
+            acc = psum.tile([P, S], F32, name="acc_a", tag="acc", bufs=5)
             for a in range(2):
                 nc.tensor.matmul_mx(out=acc[:], lhsT=w1_w[:, a, 2 * P * s:2 * P * (s + 1)].bitcast(FP4X4),
                                     lhsT_scale=w1_sc[:, a, P * s:P * (s + 1)],
@@ -174,9 +175,9 @@ def tile_list_jawari_buzz_scores_kernel(tc, tab_words, tab_scales, tab2_words, t
 
         def product_slice(b, t):
             s = PACK * b + t
-            nc.gpsimd.tensor_tensor(tanh_a[:, s, :], tanh_a[:, s, :], sines[b, t][:], ALU.mult)
+            nc.vector.tensor_tensor(tanh_a[:, s, :], tanh_a[:, s, :], sines[b, t][:], ALU.mult)
 
-        W = S // 1
+        W = S // 2
         h_rows, h_woven, h_w, h_sc = {}, {}, {}, {}
 
         def sum_slice(b, t, g):
@@ -184,7 +185,7 @@ def tile_list_jawari_buzz_scores_kernel(tc, tab_words, tab_scales, tab2_words, t
             cols = slice(W * g, W * (g + 1))
             if t == 0:
                 h_rows[b, g] = held("h_rows%d%d" % (b, g), [P, PACK, W], BF16)
-            acc = psum.tile([P, W], F32, name="acc_d", bufs=3)
+            acc = psum.tile([P, W], F32, name="acc_d", tag="acc", bufs=5)
             nc.tensor.matmul_mx(out=acc[:], lhsT=codes[key][:, P * t:P * (t + 1)].bitcast(FP8X4),
                                 lhsT_scale=scales[key][:, P * t:P * (t + 1)],
                                 rhs=v2_w[:, cols].bitcast(FP8X4), rhs_scale=v2_sc[:, cols], start=True, stop=True)
@@ -204,7 +205,7 @@ def tile_list_jawari_buzz_scores_kernel(tc, tab_words, tab_scales, tab2_words, t
 
         def score_page(c, g):
             cols = slice(W * g, W * (g + 1))
-            acc = psum.tile([P, W], F32, name="acc_y", tag="acc_d", bufs=3)
+            acc = psum.tile([P, W], F32, name="acc_y", tag="acc", bufs=5)
             for b in range(2):
                 nc.tensor.matmul_mx(out=acc[:], lhsT=w4_w[:, b, P * c:P * (c + 1)].bitcast(FP8X4),
                                     lhsT_scale=w4_sc[:, b, P * c:P * (c + 1)],
@@ -232,21 +233,21 @@ def tile_list_jawari_buzz_scores_kernel(tc, tab_words, tab_scales, tab2_words, t
             tanh_slice(PACK + t)
         v2_sc = held("v2_sc", [P, S], U8)
         nc.vector.tensor_copy(v2_sc[:], tab2_sc[:, 0, :].indirect(list2[:]))
-        v2_w = gather_words("v2_w", tab2, list2)
+        v2_w = gather_words(held("v2_w", [P, S], U32), tab2, list2)
         round_chunk(("w3", 0, 0), nc.scalar.copy)
         quantize_chunk(("w3", 0, 0))
         round_chunk(("w3", 0, 1), nc.scalar.copy)
         for t in range(PACK):
             product_slice(1, t)
         quantize_chunk(("w3", 0, 1))
-        for g in range(1):
+        for g in range(2):
             for b in range(2):
                 for t in range(PACK):
                     sum_slice(b, t, g)
-                weave_h(b, g, nc.vector.tensor_copy if b else nc.scalar.copy)
+                weave_h(b, g, nc.scalar.copy)
             for b in range(2):
                 quantize_h(b, g)
         for c in range(N // P):
-            for g in range(1):
+            for g in range(2):
                 score_page(c, g)
             nc.sync.dma_start(out[P * c:P * (c + 1), :], pages[c][:])

@@ -47,8 +47,10 @@ def tile_list_jawari_buzz_scores_kernel(tc, tab_words, tab_scales, tab2_words, t
 
         raw, codes, scales, rounded, pages = {}, {}, {}, {}, {}
 
-        def load_chunk(name, w, a, b):
-            raw[name, a, b] = held("raw_%s_%d_%d" % (name, a, b), [P, PACK, KP], F32)
+        def load_chunk(name, w, a, b, tile=None):
+            if tile is None:
+                tile = held("raw_%s_%d_%d" % (name, a, b), [P, PACK, KP], F32)
+            raw[name, a, b] = tile
             nc.sync.dma_start(raw[name, a, b][:],
                               w[KP * a:KP * (a + 1), KP * b:KP * (b + 1)].rearrange("(p j) c -> p j c", j=PACK))
 
@@ -61,13 +63,20 @@ def tile_list_jawari_buzz_scores_kernel(tc, tab_words, tab_scales, tab2_words, t
             pages[c] = held("page%d" % c, [P, T2], F32)
             nc.sync.dma_start(pages[c][:], page1[P * c:P * (c + 1), :])
 
+        follows = {("w2", 1, 1): (0,1), ("w3", 0, 0): (0,3), ("w3", 0, 1): (1,1)}
+        codes_follow = {("w2", 0, 1): (0,0)}
+
         def round_chunk(key, copy):
-            rounded[key] = ring.tile([P, PACK, P, PACK], BF16, name="rounded", align_bytes=64, bufs=3)
-            copy(rounded[key][:].rearrange("p t m j -> p m j t"),
-                 raw[key][:].rearrange("p j (m t) -> p m j t", t=PACK))
+            if key in follows:
+                rounded[key] = held("rounded_%s_%d_%d" % key, [P, PACK, P, PACK], BF16, "turns%d%d" % follows[key])
+            else:
+                rounded[key] = ring.tile([P, PACK, P, PACK], BF16, name="rounded", align_bytes=64)
+            copy(rounded[key][:].rearrange("p t m j -> p m t j"),
+                 raw[key][:].rearrange("p j (m t) -> p m t j", t=PACK))
 
         def quantize_chunk(key):
-            codes[key] = held("codes_%s_%d_%d" % key, [P, KP], U32)
+            codes[key] = held("codes_%s_%d_%d" % key, [P, KP], U32,
+                              "turns%d%d" % codes_follow[key] if key in codes_follow else None)
             scales[key] = held("scales_%s_%d_%d" % key, [P, KP], U8)
             nc.vector.quantize_mx(out=codes[key][:].bitcast(FP8X4), scales=scales[key][:],
                                   in_=rounded[key][:].rearrange("p t m j -> p (t m j)"))
@@ -84,10 +93,10 @@ def tile_list_jawari_buzz_scores_kernel(tc, tab_words, tab_scales, tab2_words, t
         zero = held("zero", [P, 1], F32)
         nc.gpsimd.memset(tab_sc_both[:, 1, :].bitcast(I32), 0)
         nc.vector.memset(tab_sc_both[:, 0, :].bitcast(I32), 0)
+        nc.vector.memset(tab2_sc[:].bitcast(I32), 0)
         nc.vector.memset(w1_sc_raw[:].bitcast(I32), 0)
         nc.vector.memset(zero[:], 0.0)
         nc.vector.memset(v_sc[:].bitcast(I32), 0)
-        nc.vector.memset(tab2_sc[:].bitcast(I32), 0)
         nc.vector.memset(w4_sc[:].bitcast(I32), 0)
 
         load_scale_rows(nc.scalar, tab_sc_both, 14, tab_scales)
@@ -99,20 +108,18 @@ def tile_list_jawari_buzz_scores_kernel(tc, tab_words, tab_scales, tab2_words, t
         nc.sync.dma_start(lists[:], offs)
         phase_sb = held("phase_sb", [P, 2, PACK], F32)
         gain_sb = held("gain_sb", [P, 2, PACK], F32)
-        load_chunk("w2", w2, 0, 0)
-        tab0 = load_table("tab0", tab_words[0])
-        load_scale_rows(nc.sync, w1_sc_raw, 0, w1_scales, range(2))
-        tab1 = load_table("tab1", tab_words[1])
-        load_scale_rows(nc.sync, w1_sc_raw, 0, w1_scales, range(2, 4))
-        load_chunk("w2", w2, 1, 0)
-        nc.sync.dma_start(phase_sb[:], phase.rearrange("(b p t) -> p b t", b=2, t=PACK))
+        nc.gpsimd.dma_start(phase_sb[:], phase.rearrange("(b p t) -> p b t", b=2, t=PACK))
+        nc.gpsimd.dma_start(gain_sb[:], gain.rearrange("(b p t) -> p b t", b=2, t=PACK))
+        load_scale_rows(nc.gpsimd, tab2_sc, 0, tab2_scales)
+        load_scale_rows(nc.gpsimd, w1_sc_raw, 0, w1_scales)
         nc.sync.dma_start(list2[:], offs2)
+        tab0 = load_table("tab0", tab_words[0])
+        load_chunk("w2", w2, 0, 0)
+        tab1 = load_table("tab1", tab_words[1])
+        load_chunk("w2", w2, 1, 0, early.tile([P, PACK, KP], F32, name="raw_shared", align_bytes=64, offset=2 * T))
         load_chunk("w2", w2, 0, 1)
-        load_scale_rows(nc.sync, tab2_sc, 0, tab2_scales, range(2))
-        load_scale_rows(nc.sync, tab2_sc, 0, tab2_scales, range(2, 4))
         load_chunk("w2", w2, 1, 1)
         tab2 = load_table("tab2", tab2_words[0])
-        nc.sync.dma_start(gain_sb[:], gain.rearrange("(b p t) -> p b t", b=2, t=PACK))
         load_chunk("w3", w3, 0, 0)
         load_chunk("w3", w3, 0, 1)
         w4_w = held("w4_w", [P, 2, N], I32)
@@ -126,8 +133,8 @@ def tile_list_jawari_buzz_scores_kernel(tc, tab_words, tab_scales, tab2_words, t
 
         w1_w = held("w1_w", [P, 2, 2 * H], U8)
         nc.vector.tensor_copy(
-            w1_w[:].bitcast(U16).rearrange("p a (b t m) -> p (a b) m t", b=2, t=PACK),
-            w1_raw[:].bitcast(U16).rearrange("p a (b m t) -> p (a b) m t", b=2, t=PACK))
+            w1_w[:].bitcast(U16).rearrange("p a (b t m) -> p (a b) t m", b=2, t=PACK),
+            w1_raw[:].bitcast(U16).rearrange("p a (b m t) -> p (a b) t m", b=2, t=PACK))
 
         tab_sc = [early.tile([P, T], U8, name="tab_sc%d" % a, align_bytes=64, offset=T * a) for a in range(2)]
         picked_sc = held("picked_sc", [P, 2, S], U8)
@@ -138,10 +145,6 @@ def tile_list_jawari_buzz_scores_kernel(tc, tab_words, tab_scales, tab2_words, t
         nc.scalar.dma_start(v_sc[0:100, :, :].bitcast(I32), picked_sc[14:114, :, :].bitcast(I32))
 
         v_w = [gather_words(early.tile([P, S], U32, name="v_w0", align_bytes=64, offset=0), tab0, lists)]
-        w1_sc = early.tile([P, 2, H], U8, name="w1_sc", align_bytes=64, offset=T)
-        nc.vector.tensor_copy(
-            w1_sc[:].rearrange("p a (b t m) -> p (a b) m t", b=2, t=PACK),
-            w1_sc_raw[:].rearrange("p a (b m t) -> p (a b) m t", b=2, t=PACK))
         v_w.append(gather_words(held("v_w1", [P, S], U32), tab1, lists))
         round_chunk(("w2", 0, 0), nc.scalar.copy)
 
@@ -166,7 +169,10 @@ def tile_list_jawari_buzz_scores_kernel(tc, tab_words, tab_scales, tab2_words, t
                                     lhsT_scale=scales[key][:, P * t:P * (t + 1)],
                                     rhs=v_w[a][:].bitcast(FP8X4), rhs_scale=v_sc[:, a, :],
                                     start=(a == 0), stop=(a == 1))
-            turns = ring.tile([P, S], I32, name="turns", bufs=3)
+            if (b, t) in list(follows.values()) + list(codes_follow.values()):
+                turns = held("turns%d%d" % (b, t), [P, S], I32)
+            else:
+                turns = ring.tile([P, S], I32, name="turns")
             nc.vector.tensor_scalar(turns[:], acc[:], phase_sb[:, b, t:t + 1], 1.0 / TWO_PI, ALU.add, ALU.mult)
             rest = ring.tile([P, S], F32, name="rest", bufs=8)
             nc.vector.scalar_tensor_tensor(rest[:], turns[:], -TWO_PI, acc[:], ALU.mult, ALU.add)
@@ -175,7 +181,7 @@ def tile_list_jawari_buzz_scores_kernel(tc, tab_words, tab_scales, tab2_words, t
 
         def product_slice(b, t):
             s = PACK * b + t
-            nc.vector.tensor_tensor(tanh_a[:, s, :], tanh_a[:, s, :], sines[b, t][:], ALU.mult)
+            nc.gpsimd.tensor_tensor(tanh_a[:, s, :], tanh_a[:, s, :], sines[b, t][:], ALU.mult)
 
         W = S // 2
         h_rows, h_woven, h_w, h_sc = {}, {}, {}, {}
@@ -216,29 +222,32 @@ def tile_list_jawari_buzz_scores_kernel(tc, tab_words, tab_scales, tab2_words, t
             nc.vector.tensor_tensor(pages[c][:].indirect(list3[:, W // 16 * g:W // 16 * (g + 1)]), scores[:],
                                     wgo_sb[:, cols], ALU.mult)
 
+        v2_sc = held("v2_sc", [P, S], U8, "tab0")
+        nc.vector.tensor_copy(v2_sc[:], tab2_sc[:, 0, :].indirect(list2[:]))
         round_chunk(("w2", 1, 0), nc.vector.tensor_copy)
         quantize_chunk(("w2", 0, 0))
         quantize_chunk(("w2", 1, 0))
+        w1_sc = early.tile([P, 2, H], U8, name="w1_sc", align_bytes=64, offset=2 * T)
+        nc.vector.tensor_copy(
+            w1_sc[:].rearrange("p a (b t m) -> p (a b) t m", b=2, t=PACK),
+            w1_sc_raw[:].rearrange("p a (b m t) -> p (a b) t m", b=2, t=PACK))
         for t in range(PACK):
             sine_slice(0, t)
             tanh_slice(t)
         round_chunk(("w2", 0, 1), nc.scalar.copy)
-        round_chunk(("w2", 1, 1), nc.scalar.copy)
-        quantize_chunk(("w2", 0, 1))
         for t in range(PACK):
             product_slice(0, t)
+        quantize_chunk(("w2", 0, 1))
+        round_chunk(("w2", 1, 1), nc.vector.tensor_copy)
         quantize_chunk(("w2", 1, 1))
+        v2_w = gather_words(held("v2_w", [P, S], U32, "raw_w2_1_1"), tab2, list2)
+        round_chunk(("w3", 0, 0), nc.scalar.copy)
         for t in range(PACK):
             sine_slice(1, t)
             tanh_slice(PACK + t)
-        v2_sc = held("v2_sc", [P, S], U8)
-        nc.vector.tensor_copy(v2_sc[:], tab2_sc[:, 0, :].indirect(list2[:]))
-        v2_w = gather_words(held("v2_w", [P, S], U32), tab2, list2)
-        round_chunk(("w3", 0, 0), nc.scalar.copy)
+            product_slice(1, t)
         quantize_chunk(("w3", 0, 0))
         round_chunk(("w3", 0, 1), nc.scalar.copy)
-        for t in range(PACK):
-            product_slice(1, t)
         quantize_chunk(("w3", 0, 1))
         for g in range(2):
             for b in range(2):

@@ -19,8 +19,16 @@ ALU = mybir.AluOpType
 
 P = 128
 PACK = 4
-KP = P * PACK
+PASS = P * PACK
+QUADRANT = 32
+LIST_ROWS = 16
 TWO_PI = 2.0 * math.pi
+SINE_BANKS = 2
+OTHER_BANKS = 8 - SINE_BANKS
+HALF = S // 2
+EARLY_PAGES = 3
+SHIFT = LIST_ROWS - 2
+SHIFTED = 3 * QUADRANT + PACK
 
 
 def tile_list_jawari_buzz_scores_kernel(tc, tab_words, tab_scales, tab2_words, tab2_scales, offs, offs2, offs3,
@@ -31,55 +39,59 @@ def tile_list_jawari_buzz_scores_kernel(tc, tab_words, tab_scales, tab2_words, t
         keep = ctx.enter_context(tc.tile_pool(name="keep", bufs=1))
         early = ctx.enter_context(tc.tile_pool(name="early", bufs=1))
         ring = ctx.enter_context(tc.tile_pool(name="ring", bufs=2))
-        psum = ctx.enter_context(tc.psum_pool(name="psum", bufs=2))
+        psum = ctx.enter_context(tc.psum_pool(name="psum", bufs=1))
 
         def held(name, shape, dtype, buffer=None):
             return keep.tile(shape, dtype, name=name, tag=buffer or name, align_bytes=64)
 
-        lists = keep.tile([P, S // 16], U16, name="lists")
-        list2 = keep.tile([P, S // 16], U16, name="list2")
-        list3 = keep.tile([P, S // 16], U16, name="list3")
+        def placed(name, shape, dtype, offset):
+            return early.tile(shape, dtype, name=name, align_bytes=64, offset=offset)
 
-        def load_scale_rows(queue, tile, first, rows, quadrants=range(4)):
-            for d in quadrants:
-                queue.dma_start(tile[32 * d + first:32 * d + first + 4, :, :].bitcast(I32),
-                                rows[:, 4 * d:4 * d + 4, :].rearrange("a q n -> q a n").bitcast(I32))
+        lists = keep.tile([P, S // LIST_ROWS], U16, name="lists")
+        list2 = keep.tile([P, S // LIST_ROWS], U16, name="list2")
+        list3 = keep.tile([P, S // LIST_ROWS], U16, name="list3")
 
-        raw, codes, scales, rounded, pages = {}, {}, {}, {}, {}
+        def load_scale_rows(queue, tile, lowest, rows):
+            for d in range(P // QUADRANT):
+                queue.dma_start(tile[QUADRANT * d + lowest:QUADRANT * d + lowest + PACK, :, :].bitcast(I32),
+                                rows[:, PACK * d:PACK * (d + 1), :].rearrange("g q n -> q g n").bitcast(I32))
 
-        def load_chunk(name, w, a, b, tile=None):
-            if tile is None:
-                tile = held("raw_%s_%d_%d" % (name, a, b), [P, PACK, KP], F32)
-            raw[name, a, b] = tile
-            nc.sync.dma_start(raw[name, a, b][:],
-                              w[KP * a:KP * (a + 1), KP * b:KP * (b + 1)].rearrange("(p j) c -> p j c", j=PACK))
+        raw, rounded, codes, scales = {}, {}, {}, {}
+
+        def load_chunk(chunk, weight, tile):
+            g, block = chunk[1:]
+            raw[chunk] = tile
+            rows = weight[PASS * g:PASS * (g + 1), PASS * block:PASS * (block + 1)]
+            nc.sync.dma_start(tile[:], rows.rearrange("(p i) c -> p i c", i=PACK))
+
+        def raw_tile(chunk):
+            return held("raw_%s_%d_%d" % chunk, [P, PACK, PASS], F32)
 
         def load_table(name, words):
             tile = held(name, [P, T], I32)
-            nc.sync.dma_start(tile[:], words.rearrange("p n t -> p (n t)").bitcast(I32))
+            nc.sync.dma_start(tile[:], words.rearrange("p n i -> p (n i)").bitcast(I32))
             return tile
 
-        def load_page(c):
-            pages[c] = held("page%d" % c, [P, T2], F32)
-            nc.sync.dma_start(pages[c][:], page1[P * c:P * (c + 1), :])
-
-        follows = {("w2", 1, 1): (0,1), ("w3", 0, 0): (0,3), ("w3", 0, 1): (1,1)}
-        codes_follow = {("w2", 0, 1): (0,0)}
-
-        def round_chunk(key, copy):
-            if key in follows:
-                rounded[key] = held("rounded_%s_%d_%d" % key, [P, PACK, P, PACK], BF16, "turns%d%d" % follows[key])
+        def round_chunk(chunk, tile, shared):
+            rounded[chunk] = tile
+            dealt = tile[:].rearrange("p t m i -> p m t i")
+            source = raw[chunk][:].rearrange("p i (m t) -> p m t i", t=PACK)
+            if shared:
+                nc.vector.tensor_copy(dealt[:, :, :PACK // 2], source[:, :, :PACK // 2])
+                nc.scalar.copy(dealt[:, :, PACK // 2:], source[:, :, PACK // 2:])
             else:
-                rounded[key] = ring.tile([P, PACK, P, PACK], BF16, name="rounded", align_bytes=64)
-            copy(rounded[key][:].rearrange("p t m j -> p m t j"),
-                 raw[key][:].rearrange("p j (m t) -> p m t j", t=PACK))
+                nc.scalar.copy(dealt, source)
 
-        def quantize_chunk(key):
-            codes[key] = held("codes_%s_%d_%d" % key, [P, KP], U32,
-                              "turns%d%d" % codes_follow[key] if key in codes_follow else None)
-            scales[key] = held("scales_%s_%d_%d" % key, [P, KP], U8)
-            nc.vector.quantize_mx(out=codes[key][:].bitcast(FP8X4), scales=scales[key][:],
-                                  in_=rounded[key][:].rearrange("p t m j -> p (t m j)"))
+        def rounded_tile(name=None, buffer=None):
+            if name is None:
+                return ring.tile([P, PACK, P, PACK], BF16, name="rounded", align_bytes=64)
+            return held(name, [P, PACK, P, PACK], BF16, buffer)
+
+        def quantize_chunk(chunk, buffer=None):
+            codes[chunk] = held("codes_%s_%d_%d" % chunk, [P, PASS], U32, buffer)
+            scales[chunk] = held("scales_%s_%d_%d" % chunk, [P, PASS], U8)
+            nc.vector.quantize_mx(out=codes[chunk][:].bitcast(FP8X4), scales=scales[chunk][:],
+                                  in_=rounded[chunk][:].rearrange("p t m i -> p (t m i)"))
 
         def gather_words(tile, table, offsets):
             nc.vector.tensor_copy(tile[:], table[:].bitcast(U32).indirect(offsets[:]))
@@ -99,164 +111,161 @@ def tile_list_jawari_buzz_scores_kernel(tc, tab_words, tab_scales, tab2_words, t
         nc.vector.memset(v_sc[:].bitcast(I32), 0)
         nc.vector.memset(w4_sc[:].bitcast(I32), 0)
 
-        load_scale_rows(nc.scalar, tab_sc_both, 14, tab_scales)
+        load_scale_rows(nc.scalar, tab_sc_both, SHIFT, tab_scales)
         unread = held("unread", [P, 1], F32)
         nc.scalar.activation(unread[:], zero[:], ACT.Silu)
 
-        w1_raw = early.tile([P, 2, 2 * H], U8, name="w1_raw", align_bytes=64, offset=0)
-        nc.sync.dma_start(w1_raw[:].bitcast(I32), w1_words.rearrange("a p n -> p a n").bitcast(I32))
+        w1_raw = placed("w1_raw", [P, 2, 2 * H], U8, 0)
+        nc.sync.dma_start(w1_raw[:].bitcast(I32), w1_words.rearrange("g p n -> p g n").bitcast(I32))
         nc.sync.dma_start(lists[:], offs)
         phase_sb = held("phase_sb", [P, 2, PACK], F32)
         gain_sb = held("gain_sb", [P, 2, PACK], F32)
-        nc.gpsimd.dma_start(phase_sb[:], phase.rearrange("(b p t) -> p b t", b=2, t=PACK))
-        nc.gpsimd.dma_start(gain_sb[:], gain.rearrange("(b p t) -> p b t", b=2, t=PACK))
+        nc.gpsimd.dma_start(phase_sb[:], phase.rearrange("(B p t) -> p B t", B=2, t=PACK))
+        nc.gpsimd.dma_start(gain_sb[:], gain.rearrange("(B p t) -> p B t", B=2, t=PACK))
         load_scale_rows(nc.gpsimd, tab2_sc, 0, tab2_scales)
         load_scale_rows(nc.gpsimd, w1_sc_raw, 0, w1_scales)
         nc.sync.dma_start(list2[:], offs2)
         tab0 = load_table("tab0", tab_words[0])
-        load_chunk("w2", w2, 0, 0)
+        load_chunk(("w2", 0, 0), w2, raw_tile(("w2", 0, 0)))
         tab1 = load_table("tab1", tab_words[1])
-        load_chunk("w2", w2, 1, 0, early.tile([P, PACK, KP], F32, name="raw_shared", align_bytes=64, offset=2 * T))
-        load_chunk("w2", w2, 0, 1)
-        load_chunk("w2", w2, 1, 1)
+        load_chunk(("w2", 1, 0), w2, placed("raw_w2_1_0", [P, PACK, PASS], F32, 2 * T))
+        load_chunk(("w2", 0, 1), w2, raw_tile(("w2", 0, 1)))
+        load_chunk(("w2", 1, 1), w2, raw_tile(("w2", 1, 1)))
         tab2 = load_table("tab2", tab2_words[0])
-        load_chunk("w3", w3, 0, 0)
-        load_chunk("w3", w3, 0, 1)
+        load_chunk(("w3", 0, 0), w3, raw_tile(("w3", 0, 0)))
+        load_chunk(("w3", 0, 1), w3, raw_tile(("w3", 0, 1)))
         w4_w = held("w4_w", [P, 2, N], I32)
-        nc.sync.dma_start(w4_w[:], w4_words.rearrange("a p n t -> p a (n t)").bitcast(I32))
+        nc.sync.dma_start(w4_w[:], w4_words.rearrange("g p n i -> p g (n i)").bitcast(I32))
         load_scale_rows(nc.sync, w4_sc, 0, w4_scales)
         nc.sync.dma_start(list3[:], offs3)
         wgo_sb = held("wgo_sb", [P, S], F32)
         nc.sync.dma_start(wgo_sb[:], wgo)
-        for c in range(N // P):
-            load_page(c)
+        pages = [held("page%d" % c, [P, T2], F32) for c in range(N // P)]
+        for c, page in enumerate(pages):
+            nc.sync.dma_start(page[:], page1[P * c:P * (c + 1), :])
 
         w1_w = held("w1_w", [P, 2, 2 * H], U8)
         nc.vector.tensor_copy(
-            w1_w[:].bitcast(U16).rearrange("p a (b t m) -> p (a b) t m", b=2, t=PACK),
-            w1_raw[:].bitcast(U16).rearrange("p a (b m t) -> p (a b) t m", b=2, t=PACK))
+            w1_w[:].bitcast(U16).rearrange("p g (B t m) -> p (g B) t m", B=2, t=PACK),
+            w1_raw[:].bitcast(U16).rearrange("p g (B m t) -> p (g B) t m", B=2, t=PACK))
 
-        tab_sc = [early.tile([P, T], U8, name="tab_sc%d" % a, align_bytes=64, offset=T * a) for a in range(2)]
+        tab_sc = [placed("tab_sc%d" % g, [P, T], U8, T * g) for g in range(2)]
         picked_sc = held("picked_sc", [P, 2, S], U8)
-        for a in range(2):
-            nc.vector.tensor_copy(tab_sc[a][:].bitcast(I32), tab_sc_both[:, a, :].bitcast(I32))
-        for a in range(2):
-            nc.vector.tensor_copy(picked_sc[:, a, :], tab_sc[a][:].indirect(lists[:]))
-        nc.scalar.dma_start(v_sc[0:100, :, :].bitcast(I32), picked_sc[14:114, :, :].bitcast(I32))
+        for g in range(2):
+            nc.vector.tensor_copy(tab_sc[g][:].bitcast(I32), tab_sc_both[:, g, :].bitcast(I32))
+        for g in range(2):
+            nc.vector.tensor_copy(picked_sc[:, g, :], tab_sc[g][:].indirect(lists[:]))
+        nc.scalar.dma_start(v_sc[0:SHIFTED, :, :].bitcast(I32),
+                            picked_sc[SHIFT:SHIFT + SHIFTED, :, :].bitcast(I32))
 
-        v_w = [gather_words(early.tile([P, S], U32, name="v_w0", align_bytes=64, offset=0), tab0, lists)]
-        v_w.append(gather_words(held("v_w1", [P, S], U32), tab1, lists))
-        round_chunk(("w2", 0, 0), nc.scalar.copy)
+        v_w = [gather_words(placed("v_w0", [P, S], U32, 0), tab0, lists),
+               gather_words(held("v_w1", [P, S], U32), tab1, lists)]
+        round_chunk(("w2", 0, 0), rounded_tile(), False)
 
-        tanh_a = held("tanh_a", [P, 2 * PACK, S], F32)
-
-        def tanh_slice(s):
-            acc = psum.tile([P, S], F32, name="acc_a", tag="acc", bufs=5)
-            for a in range(2):
-                nc.tensor.matmul_mx(out=acc[:], lhsT=w1_w[:, a, 2 * P * s:2 * P * (s + 1)].bitcast(FP4X4),
-                                    lhsT_scale=w1_sc[:, a, P * s:P * (s + 1)],
-                                    rhs=v_w[a][:].bitcast(FP8X4), rhs_scale=v_sc[:, a, :],
-                                    start=(a == 0), stop=(a == 1))
-            nc.scalar.activation(tanh_a[:, s, :], acc[:], ACT.Tanh)
-
+        buzz = held("buzz", [P, 2 * PACK, S], F32)
         sines = {}
 
-        def sine_slice(b, t):
-            acc = psum.tile([P, S], F32, name="acc_b", bufs=3)
-            for a in range(2):
-                key = ("w2", a, b)
-                nc.tensor.matmul_mx(out=acc[:], lhsT=codes[key][:, P * t:P * (t + 1)].bitcast(FP8X4),
-                                    lhsT_scale=scales[key][:, P * t:P * (t + 1)],
-                                    rhs=v_w[a][:].bitcast(FP8X4), rhs_scale=v_sc[:, a, :],
-                                    start=(a == 0), stop=(a == 1))
-            if (b, t) in list(follows.values()) + list(codes_follow.values()):
-                turns = held("turns%d%d" % (b, t), [P, S], I32)
-            else:
-                turns = ring.tile([P, S], I32, name="turns")
-            nc.vector.tensor_scalar(turns[:], acc[:], phase_sb[:, b, t:t + 1], 1.0 / TWO_PI, ALU.add, ALU.mult)
-            rest = ring.tile([P, S], F32, name="rest", bufs=8)
-            nc.vector.scalar_tensor_tensor(rest[:], turns[:], -TWO_PI, acc[:], ALU.mult, ALU.add)
-            sines[b, t] = rest
-            nc.scalar.activation(sines[b, t][:], rest[:], ACT.Sin, bias=phase_sb[:, b, t:t + 1])
+        def tanh_slice(block, t):
+            s = PACK * block + t
+            acc = psum.tile([P, S], F32, name="acc_a", tag="acc", bufs=OTHER_BANKS)
+            for g in range(2):
+                nc.tensor.matmul_mx(out=acc[:], lhsT=w1_w[:, g, 2 * P * s:2 * P * (s + 1)].bitcast(FP4X4),
+                                    lhsT_scale=w1_sc[:, g, P * s:P * (s + 1)],
+                                    rhs=v_w[g][:].bitcast(FP8X4), rhs_scale=v_sc[:, g, :],
+                                    start=(g == 0), stop=(g == 1))
+            nc.scalar.activation(buzz[:, s, :], acc[:], ACT.Tanh)
 
-        def product_slice(b, t):
-            s = PACK * b + t
-            nc.gpsimd.tensor_tensor(tanh_a[:, s, :], tanh_a[:, s, :], sines[b, t][:], ALU.mult)
+        def sine_slice(block, t, turns):
+            acc = psum.tile([P, S], F32, name="acc_b", bufs=SINE_BANKS)
+            for g in range(2):
+                chunk = ("w2", g, block)
+                nc.tensor.matmul_mx(out=acc[:], lhsT=codes[chunk][:, P * t:P * (t + 1)].bitcast(FP8X4),
+                                    lhsT_scale=scales[chunk][:, P * t:P * (t + 1)],
+                                    rhs=v_w[g][:].bitcast(FP8X4), rhs_scale=v_sc[:, g, :],
+                                    start=(g == 0), stop=(g == 1))
+            row_phase = phase_sb[:, block, t:t + 1]
+            nc.vector.tensor_scalar(turns[:], acc[:], row_phase, 1.0 / TWO_PI, ALU.add, ALU.mult)
+            sine = ring.tile([P, S], F32, name="sine", bufs=2 * PACK)
+            nc.vector.scalar_tensor_tensor(sine[:], turns[:], -TWO_PI, acc[:], ALU.mult, ALU.add)
+            nc.scalar.activation(sine[:], sine[:], ACT.Sin, bias=row_phase)
+            sines[block, t] = sine
 
-        W = S // 2
-        h_rows, h_woven, h_w, h_sc = {}, {}, {}, {}
+        def product_slice(block, t):
+            s = PACK * block + t
+            nc.gpsimd.tensor_tensor(buzz[:, s, :], buzz[:, s, :], sines[block, t][:], ALU.mult)
 
-        def sum_slice(b, t, g):
-            key = ("w3", 0, b)
-            cols = slice(W * g, W * (g + 1))
-            if t == 0:
-                h_rows[b, g] = held("h_rows%d%d" % (b, g), [P, PACK, W], BF16)
-            acc = psum.tile([P, W], F32, name="acc_d", tag="acc", bufs=5)
-            nc.tensor.matmul_mx(out=acc[:], lhsT=codes[key][:, P * t:P * (t + 1)].bitcast(FP8X4),
-                                lhsT_scale=scales[key][:, P * t:P * (t + 1)],
-                                rhs=v2_w[:, cols].bitcast(FP8X4), rhs_scale=v2_sc[:, cols], start=True, stop=True)
-            nc.vector.scalar_tensor_tensor(h_rows[b, g][:, t, :], tanh_a[:, PACK * b + t, cols], gain_sb[:, b, t:t + 1],
-                                           acc[:], ALU.mult, ALU.add)
+        h_w = [held("h_w%d" % block, [P, S], U32) for block in range(2)]
+        h_sc = [held("h_sc%d" % block, [P, S], U8) for block in range(2)]
+        woven = {}
 
-        def weave_h(b, g, copy):
-            h_woven[b, g] = held("h_woven%d%d" % (b, g), [P, W, PACK], BF16)
-            copy(h_woven[b, g][:].rearrange("p (c i) t -> p c t i", i=4),
-                 h_rows[b, g][:].rearrange("p t (c i) -> p c t i", i=4))
+        def sum_and_weave(block, cols):
+            chunk = ("w3", 0, block)
+            h_rows = held("h_rows%d_%d" % (block, cols.start), [P, PACK, HALF], BF16)
+            for t in range(PACK):
+                acc = psum.tile([P, HALF], F32, name="acc_d", tag="acc", bufs=OTHER_BANKS)
+                nc.tensor.matmul_mx(out=acc[:], lhsT=codes[chunk][:, P * t:P * (t + 1)].bitcast(FP8X4),
+                                    lhsT_scale=scales[chunk][:, P * t:P * (t + 1)],
+                                    rhs=v2_w[:, cols].bitcast(FP8X4), rhs_scale=v2_sc[:, cols],
+                                    start=True, stop=True)
+                nc.vector.scalar_tensor_tensor(h_rows[:, t, :], buzz[:, PACK * block + t, cols],
+                                               gain_sb[:, block, t:t + 1], acc[:], ALU.mult, ALU.add)
+            woven[block] = held("woven%d_%d" % (block, cols.start), [P, HALF, PACK], BF16)
+            nc.scalar.copy(woven[block][:].rearrange("p (c n) t -> p c t n", n=4),
+                           h_rows[:].rearrange("p t (c n) -> p c t n", n=4))
 
-        def quantize_h(b, g):
-            h_w[b, g] = held("h_w%d%d" % (b, g), [P, W], U32)
-            h_sc[b, g] = held("h_sc%d%d" % (b, g), [P, W], U8)
-            nc.vector.quantize_mx(out=h_w[b, g][:].bitcast(FP8X4), scales=h_sc[b, g][:],
-                                  in_=h_woven[b, g][:].rearrange("p n t -> p (n t)"))
-
-        def score_page(c, g):
-            cols = slice(W * g, W * (g + 1))
-            acc = psum.tile([P, W], F32, name="acc_y", tag="acc", bufs=5)
-            for b in range(2):
-                nc.tensor.matmul_mx(out=acc[:], lhsT=w4_w[:, b, P * c:P * (c + 1)].bitcast(FP8X4),
-                                    lhsT_scale=w4_sc[:, b, P * c:P * (c + 1)],
-                                    rhs=h_w[b, g][:].bitcast(FP8X4), rhs_scale=h_sc[b, g][:],
-                                    start=(b == 0), stop=(b == 1))
-            scores = ring.tile([P, W], F32, name="scores", bufs=3)
+        def score_page(c, cols):
+            width = cols.stop - cols.start
+            acc = psum.tile([P, width], F32, name="acc_y", tag="acc", bufs=OTHER_BANKS)
+            for block in range(2):
+                nc.tensor.matmul_mx(out=acc[:], lhsT=w4_w[:, block, P * c:P * (c + 1)].bitcast(FP8X4),
+                                    lhsT_scale=w4_sc[:, block, P * c:P * (c + 1)],
+                                    rhs=h_w[block][:, cols].bitcast(FP8X4), rhs_scale=h_sc[block][:, cols],
+                                    start=(block == 0), stop=(block == 1))
+            scores = ring.tile([P, width], F32, name="scores", bufs=3)
             nc.scalar.copy(scores[:], acc[:])
-            nc.vector.tensor_tensor(pages[c][:].indirect(list3[:, W // 16 * g:W // 16 * (g + 1)]), scores[:],
-                                    wgo_sb[:, cols], ALU.mult)
+            places = list3[:, cols.start // LIST_ROWS:cols.stop // LIST_ROWS]
+            nc.vector.tensor_tensor(pages[c][:].indirect(places), scores[:], wgo_sb[:, cols], ALU.mult)
 
         v2_sc = held("v2_sc", [P, S], U8, "tab0")
         nc.vector.tensor_copy(v2_sc[:], tab2_sc[:, 0, :].indirect(list2[:]))
-        round_chunk(("w2", 1, 0), nc.vector.tensor_copy)
+        round_chunk(("w2", 1, 0), rounded_tile(), True)
         quantize_chunk(("w2", 0, 0))
         quantize_chunk(("w2", 1, 0))
-        w1_sc = early.tile([P, 2, H], U8, name="w1_sc", align_bytes=64, offset=2 * T)
+        w1_sc = placed("w1_sc", [P, 2, H], U8, 2 * T)
         nc.vector.tensor_copy(
-            w1_sc[:].rearrange("p a (b t m) -> p (a b) t m", b=2, t=PACK),
-            w1_sc_raw[:].rearrange("p a (b m t) -> p (a b) t m", b=2, t=PACK))
+            w1_sc[:].rearrange("p g (B t m) -> p (g B) t m", B=2, t=PACK),
+            w1_sc_raw[:].rearrange("p g (B m t) -> p (g B) t m", B=2, t=PACK))
+
         for t in range(PACK):
-            sine_slice(0, t)
-            tanh_slice(t)
-        round_chunk(("w2", 0, 1), nc.scalar.copy)
+            sine_slice(0, t, held("turns%d" % t, [P, S], I32))
+            tanh_slice(0, t)
+        round_chunk(("w2", 0, 1), rounded_tile(), False)
         for t in range(PACK):
             product_slice(0, t)
-        quantize_chunk(("w2", 0, 1))
-        round_chunk(("w2", 1, 1), nc.vector.tensor_copy)
+        quantize_chunk(("w2", 0, 1), "turns0")
+        round_chunk(("w2", 1, 1), rounded_tile("rounded_w2_1_1", "turns1"), True)
         quantize_chunk(("w2", 1, 1))
         v2_w = gather_words(held("v2_w", [P, S], U32, "raw_w2_1_1"), tab2, list2)
-        round_chunk(("w3", 0, 0), nc.scalar.copy)
+        round_chunk(("w3", 0, 0), rounded_tile("rounded_w3_0_0", "turns2"), False)
+
         for t in range(PACK):
-            sine_slice(1, t)
-            tanh_slice(PACK + t)
+            sine_slice(1, t, ring.tile([P, S], I32, name="turns"))
+            tanh_slice(1, t)
             product_slice(1, t)
         quantize_chunk(("w3", 0, 0))
-        round_chunk(("w3", 0, 1), nc.scalar.copy)
+        round_chunk(("w3", 0, 1), rounded_tile("rounded_w3_0_1", "turns3"), True)
         quantize_chunk(("w3", 0, 1))
-        for g in range(2):
-            for b in range(2):
-                for t in range(PACK):
-                    sum_slice(b, t, g)
-                weave_h(b, g, nc.scalar.copy)
-            for b in range(2):
-                quantize_h(b, g)
-        for c in range(N // P):
-            for g in range(2):
-                score_page(c, g)
-            nc.sync.dma_start(out[P * c:P * (c + 1), :], pages[c][:])
+
+        first, second = slice(0, HALF), slice(HALF, S)
+        for cols in (first, second):
+            for block in range(2):
+                sum_and_weave(block, cols)
+            for block in range(2):
+                nc.vector.quantize_mx(out=h_w[block][:, cols].bitcast(FP8X4), scales=h_sc[block][:, cols],
+                                      in_=woven[block][:].rearrange("p n t -> p (n t)"))
+
+        for c in range(EARLY_PAGES):
+            score_page(c, first)
+        for c, page in enumerate(pages):
+            score_page(c, second if c < EARLY_PAGES else slice(0, S))
+            nc.sync.dma_start(out[P * c:P * (c + 1), :], page[:])

import math
from contextlib import ExitStack

import concourse.mybir as mybir

K, K2, H, N, T, S, T2 = 1024, 512, 1024, 768, 2048, 512, 1024
FLOPS = 2 * S * (2 * K * H + K2 * H + H * N)

F32 = mybir.dt.float32
BF16 = mybir.dt.bfloat16
I32 = mybir.dt.int32
U32 = mybir.dt.uint32
U16 = mybir.dt.uint16
U8 = mybir.dt.uint8
FP8X4 = mybir.dt.float8_e4m3fn_x4
FP4X4 = mybir.dt.float4_e2m1fn_x4
ACT = mybir.ActivationFunctionType
ALU = mybir.AluOpType

P = 128
PACK = 4
PASS = P * PACK
QUADRANT = 32
LIST_ROWS = 16
TWO_PI = 2.0 * math.pi
SINE_BANKS = 2
OTHER_BANKS = 8 - SINE_BANKS
HALF = S // 2
EARLY_PAGES = 3
SHIFT = LIST_ROWS - 2
SHIFTED = 3 * QUADRANT + PACK


def tile_list_jawari_buzz_scores_kernel(tc, tab_words, tab_scales, tab2_words, tab2_scales, offs, offs2, offs3,
                                                  w1_words, w1_scales, w2, phase, gain, w3, w4_words, w4_scales,
                                                  page1, wgo, out):
    nc = tc.nc
    with ExitStack() as ctx:
        keep = ctx.enter_context(tc.tile_pool(name="keep", bufs=1))
        early = ctx.enter_context(tc.tile_pool(name="early", bufs=1))
        ring = ctx.enter_context(tc.tile_pool(name="ring", bufs=2))
        psum = ctx.enter_context(tc.psum_pool(name="psum", bufs=1))

        def held(name, shape, dtype, buffer=None):
            return keep.tile(shape, dtype, name=name, tag=buffer or name, align_bytes=64)

        def placed(name, shape, dtype, offset):
            return early.tile(shape, dtype, name=name, align_bytes=64, offset=offset)

        lists = keep.tile([P, S // LIST_ROWS], U16, name="lists")
        list2 = keep.tile([P, S // LIST_ROWS], U16, name="list2")
        list3 = keep.tile([P, S // LIST_ROWS], U16, name="list3")

        def load_scale_rows(queue, tile, lowest, rows):
            for d in range(P // QUADRANT):
                queue.dma_start(tile[QUADRANT * d + lowest:QUADRANT * d + lowest + PACK, :, :].bitcast(I32),
                                rows[:, PACK * d:PACK * (d + 1), :].rearrange("g q n -> q g n").bitcast(I32))

        raw, rounded, codes, scales = {}, {}, {}, {}

        def load_chunk(chunk, weight, tile):
            g, block = chunk[1:]
            raw[chunk] = tile
            rows = weight[PASS * g:PASS * (g + 1), PASS * block:PASS * (block + 1)]
            nc.sync.dma_start(tile[:], rows.rearrange("(p i) c -> p i c", i=PACK))

        def raw_tile(chunk):
            return held("raw_%s_%d_%d" % chunk, [P, PACK, PASS], F32)

        def load_table(name, words):
            tile = held(name, [P, T], I32)
            nc.sync.dma_start(tile[:], words.rearrange("p n i -> p (n i)").bitcast(I32))
            return tile

        def round_chunk(chunk, tile, shared):
            rounded[chunk] = tile
            dealt = tile[:].rearrange("p t m i -> p m t i")
            source = raw[chunk][:].rearrange("p i (m t) -> p m t i", t=PACK)
            if shared:
                nc.vector.tensor_copy(dealt[:, :, :PACK // 2], source[:, :, :PACK // 2])
                nc.scalar.copy(dealt[:, :, PACK // 2:], source[:, :, PACK // 2:])
            else:
                nc.scalar.copy(dealt, source)

        def rounded_tile(name=None, buffer=None):
            if name is None:
                return ring.tile([P, PACK, P, PACK], BF16, name="rounded", align_bytes=64)
            return held(name, [P, PACK, P, PACK], BF16, buffer)

        def quantize_chunk(chunk, buffer=None):
            codes[chunk] = held("codes_%s_%d_%d" % chunk, [P, PASS], U32, buffer)
            scales[chunk] = held("scales_%s_%d_%d" % chunk, [P, PASS], U8)
            nc.vector.quantize_mx(out=codes[chunk][:].bitcast(FP8X4), scales=scales[chunk][:],
                                  in_=rounded[chunk][:].rearrange("p t m i -> p (t m i)"))

        def gather_words(tile, table, offsets):
            nc.vector.tensor_copy(tile[:], table[:].bitcast(U32).indirect(offsets[:]))
            return tile

        tab_sc_both = held("tab_sc_both", [P, 2, T], U8)
        w1_sc_raw = held("w1_sc_raw", [P, 2, H], U8)
        tab2_sc = held("tab2_sc", [P, 1, T], U8)
        w4_sc = held("w4_sc", [P, 2, N], U8)
        v_sc = held("v_sc", [P, 2, S], U8)
        zero = held("zero", [P, 1], F32)
        nc.gpsimd.memset(tab_sc_both[:, 1, :].bitcast(I32), 0)
        nc.vector.memset(tab_sc_both[:, 0, :].bitcast(I32), 0)
        nc.vector.memset(tab2_sc[:].bitcast(I32), 0)
        nc.vector.memset(w1_sc_raw[:].bitcast(I32), 0)
        nc.vector.memset(zero[:], 0.0)
        nc.vector.memset(v_sc[:].bitcast(I32), 0)
        nc.vector.memset(w4_sc[:].bitcast(I32), 0)

        load_scale_rows(nc.scalar, tab_sc_both, SHIFT, tab_scales)
        unread = held("unread", [P, 1], F32)
        nc.scalar.activation(unread[:], zero[:], ACT.Silu)

        w1_raw = placed("w1_raw", [P, 2, 2 * H], U8, 0)
        nc.sync.dma_start(w1_raw[:].bitcast(I32), w1_words.rearrange("g p n -> p g n").bitcast(I32))
        nc.sync.dma_start(lists[:], offs)
        phase_sb = held("phase_sb", [P, 2, PACK], F32)
        gain_sb = held("gain_sb", [P, 2, PACK], F32)
        nc.gpsimd.dma_start(phase_sb[:], phase.rearrange("(B p t) -> p B t", B=2, t=PACK))
        nc.gpsimd.dma_start(gain_sb[:], gain.rearrange("(B p t) -> p B t", B=2, t=PACK))
        load_scale_rows(nc.gpsimd, tab2_sc, 0, tab2_scales)
        load_scale_rows(nc.gpsimd, w1_sc_raw, 0, w1_scales)
        nc.sync.dma_start(list2[:], offs2)
        tab0 = load_table("tab0", tab_words[0])
        load_chunk(("w2", 0, 0), w2, raw_tile(("w2", 0, 0)))
        tab1 = load_table("tab1", tab_words[1])
        load_chunk(("w2", 1, 0), w2, placed("raw_w2_1_0", [P, PACK, PASS], F32, 2 * T))
        load_chunk(("w2", 0, 1), w2, raw_tile(("w2", 0, 1)))
        load_chunk(("w2", 1, 1), w2, raw_tile(("w2", 1, 1)))
        tab2 = load_table("tab2", tab2_words[0])
        load_chunk(("w3", 0, 0), w3, raw_tile(("w3", 0, 0)))
        load_chunk(("w3", 0, 1), w3, raw_tile(("w3", 0, 1)))
        w4_w = held("w4_w", [P, 2, N], I32)
        nc.sync.dma_start(w4_w[:], w4_words.rearrange("g p n i -> p g (n i)").bitcast(I32))
        load_scale_rows(nc.sync, w4_sc, 0, w4_scales)
        nc.sync.dma_start(list3[:], offs3)
        wgo_sb = held("wgo_sb", [P, S], F32)
        nc.sync.dma_start(wgo_sb[:], wgo)
        pages = [held("page%d" % c, [P, T2], F32) for c in range(N // P)]
        for c, page in enumerate(pages):
            nc.sync.dma_start(page[:], page1[P * c:P * (c + 1), :])

        w1_w = held("w1_w", [P, 2, 2 * H], U8)
        nc.vector.tensor_copy(
            w1_w[:].bitcast(U16).rearrange("p g (B t m) -> p (g B) t m", B=2, t=PACK),
            w1_raw[:].bitcast(U16).rearrange("p g (B m t) -> p (g B) t m", B=2, t=PACK))

        tab_sc = [placed("tab_sc%d" % g, [P, T], U8, T * g) for g in range(2)]
        picked_sc = held("picked_sc", [P, 2, S], U8)
        for g in range(2):
            nc.vector.tensor_copy(tab_sc[g][:].bitcast(I32), tab_sc_both[:, g, :].bitcast(I32))
        for g in range(2):
            nc.vector.tensor_copy(picked_sc[:, g, :], tab_sc[g][:].indirect(lists[:]))
        nc.scalar.dma_start(v_sc[0:SHIFTED, :, :].bitcast(I32),
                            picked_sc[SHIFT:SHIFT + SHIFTED, :, :].bitcast(I32))

        v_w = [gather_words(placed("v_w0", [P, S], U32, 0), tab0, lists),
               gather_words(held("v_w1", [P, S], U32), tab1, lists)]
        round_chunk(("w2", 0, 0), rounded_tile(), False)

        buzz = held("buzz", [P, 2 * PACK, S], F32)
        sines = {}

        def tanh_slice(block, t):
            s = PACK * block + t
            acc = psum.tile([P, S], F32, name="acc_a", tag="acc", bufs=OTHER_BANKS)
            for g in range(2):
                nc.tensor.matmul_mx(out=acc[:], lhsT=w1_w[:, g, 2 * P * s:2 * P * (s + 1)].bitcast(FP4X4),
                                    lhsT_scale=w1_sc[:, g, P * s:P * (s + 1)],
                                    rhs=v_w[g][:].bitcast(FP8X4), rhs_scale=v_sc[:, g, :],
                                    start=(g == 0), stop=(g == 1))
            nc.scalar.activation(buzz[:, s, :], acc[:], ACT.Tanh)

        def sine_slice(block, t, turns):
            acc = psum.tile([P, S], F32, name="acc_b", bufs=SINE_BANKS)
            for g in range(2):
                chunk = ("w2", g, block)
                nc.tensor.matmul_mx(out=acc[:], lhsT=codes[chunk][:, P * t:P * (t + 1)].bitcast(FP8X4),
                                    lhsT_scale=scales[chunk][:, P * t:P * (t + 1)],
                                    rhs=v_w[g][:].bitcast(FP8X4), rhs_scale=v_sc[:, g, :],
                                    start=(g == 0), stop=(g == 1))
            row_phase = phase_sb[:, block, t:t + 1]
            nc.vector.tensor_scalar(turns[:], acc[:], row_phase, 1.0 / TWO_PI, ALU.add, ALU.mult)
            sine = ring.tile([P, S], F32, name="sine", bufs=2 * PACK)
            nc.vector.scalar_tensor_tensor(sine[:], turns[:], -TWO_PI, acc[:], ALU.mult, ALU.add)
            nc.scalar.activation(sine[:], sine[:], ACT.Sin, bias=row_phase)
            sines[block, t] = sine

        def product_slice(block, t):
            s = PACK * block + t
            nc.gpsimd.tensor_tensor(buzz[:, s, :], buzz[:, s, :], sines[block, t][:], ALU.mult)

        h_w = [held("h_w%d" % block, [P, S], U32) for block in range(2)]
        h_sc = [held("h_sc%d" % block, [P, S], U8) for block in range(2)]
        woven = {}

        def sum_and_weave(block, cols):
            chunk = ("w3", 0, block)
            h_rows = held("h_rows%d_%d" % (block, cols.start), [P, PACK, HALF], BF16)
            for t in range(PACK):
                acc = psum.tile([P, HALF], F32, name="acc_d", tag="acc", bufs=OTHER_BANKS)
                nc.tensor.matmul_mx(out=acc[:], lhsT=codes[chunk][:, P * t:P * (t + 1)].bitcast(FP8X4),
                                    lhsT_scale=scales[chunk][:, P * t:P * (t + 1)],
                                    rhs=v2_w[:, cols].bitcast(FP8X4), rhs_scale=v2_sc[:, cols],
                                    start=True, stop=True)
                nc.vector.scalar_tensor_tensor(h_rows[:, t, :], buzz[:, PACK * block + t, cols],
                                               gain_sb[:, block, t:t + 1], acc[:], ALU.mult, ALU.add)
            woven[block] = held("woven%d_%d" % (block, cols.start), [P, HALF, PACK], BF16)
            nc.scalar.copy(woven[block][:].rearrange("p (c n) t -> p c t n", n=4),
                           h_rows[:].rearrange("p t (c n) -> p c t n", n=4))

        def score_page(c, cols):
            width = cols.stop - cols.start
            acc = psum.tile([P, width], F32, name="acc_y", tag="acc", bufs=OTHER_BANKS)
            for block in range(2):
                nc.tensor.matmul_mx(out=acc[:], lhsT=w4_w[:, block, P * c:P * (c + 1)].bitcast(FP8X4),
                                    lhsT_scale=w4_sc[:, block, P * c:P * (c + 1)],
                                    rhs=h_w[block][:, cols].bitcast(FP8X4), rhs_scale=h_sc[block][:, cols],
                                    start=(block == 0), stop=(block == 1))
            scores = ring.tile([P, width], F32, name="scores", bufs=3)
            nc.scalar.copy(scores[:], acc[:])
            places = list3[:, cols.start // LIST_ROWS:cols.stop // LIST_ROWS]
            nc.vector.tensor_tensor(pages[c][:].indirect(places), scores[:], wgo_sb[:, cols], ALU.mult)

        v2_sc = held("v2_sc", [P, S], U8, "tab0")
        nc.vector.tensor_copy(v2_sc[:], tab2_sc[:, 0, :].indirect(list2[:]))
        round_chunk(("w2", 1, 0), rounded_tile(), True)
        quantize_chunk(("w2", 0, 0))
        quantize_chunk(("w2", 1, 0))
        w1_sc = placed("w1_sc", [P, 2, H], U8, 2 * T)
        nc.vector.tensor_copy(
            w1_sc[:].rearrange("p g (B t m) -> p (g B) t m", B=2, t=PACK),
            w1_sc_raw[:].rearrange("p g (B m t) -> p (g B) t m", B=2, t=PACK))

        for t in range(PACK):
            sine_slice(0, t, held("turns%d" % t, [P, S], I32))
            tanh_slice(0, t)
        round_chunk(("w2", 0, 1), rounded_tile(), False)
        for t in range(PACK):
            product_slice(0, t)
        quantize_chunk(("w2", 0, 1), "turns0")
        round_chunk(("w2", 1, 1), rounded_tile("rounded_w2_1_1", "turns1"), True)
        quantize_chunk(("w2", 1, 1))
        v2_w = gather_words(held("v2_w", [P, S], U32, "raw_w2_1_1"), tab2, list2)
        round_chunk(("w3", 0, 0), rounded_tile("rounded_w3_0_0", "turns2"), False)

        for t in range(PACK):
            sine_slice(1, t, ring.tile([P, S], I32, name="turns"))
            tanh_slice(1, t)
            product_slice(1, t)
        quantize_chunk(("w3", 0, 0))
        round_chunk(("w3", 0, 1), rounded_tile("rounded_w3_0_1", "turns3"), True)
        quantize_chunk(("w3", 0, 1))

        first, second = slice(0, HALF), slice(HALF, S)
        for cols in (first, second):
            for block in range(2):
                sum_and_weave(block, cols)
            for block in range(2):
                nc.vector.quantize_mx(out=h_w[block][:, cols].bitcast(FP8X4), scales=h_sc[block][:, cols],
                                      in_=woven[block][:].rearrange("p n t -> p (n t)"))

        for c in range(EARLY_PAGES):
            score_page(c, first)
        for c, page in enumerate(pages):
            score_page(c, second if c < EARLY_PAGES else slice(0, S))
            nc.sync.dma_start(out[P * c:P * (c + 1), :], page[:])
